import numpy as np, ml_dtypes
CORES = [16,18,20,22]
N = 4
BF = ml_dtypes.bfloat16
def gentries(a):
    return np.ascontiguousarray(a.reshape(8, 16, -1).transpose(0, 2, 1)).reshape(8, -1)
def gtable(e):
    e = np.asarray(e); return np.ascontiguousarray(e.reshape(8, -1, 16).transpose(0, 2, 1)).reshape(128, -1).astype(np.int32)
V, G, H, Q, ST = 3072, 1024, 1, 3, 3
W = V + H * G
def come(v, snd):
    return np.concatenate([np.take_along_axis(np.roll(v, -d, axis=0), np.roll(snd[:, :, d - 1], -d, axis=0), 2) for d in range(1, H + 1)], axis=2)
def some(rng):
    return np.ascontiguousarray(np.argsort(rng.random((N, 8, H, V)), axis=-1)[..., :G])
def traffic(rng):
    snd = some(rng); pace = rng.permutation(np.array([2, 3, 4, 4, 6, 8, 8, 16])).reshape(1, 8, 1)
    base = 64 + (rng.random((N, 8, V)) * W * pace).astype(np.int64)
    lane = (rng.random((N, 8, V)) < 0.3 + 0.4 * rng.random((1, 8, 1))).astype(np.int64)
    pw = np.concatenate([base, come(base, snd)], axis=2); lw = np.concatenate([lane, come(lane, snd)], axis=2)
    la = np.zeros((N, 8, V), np.int64); lb = np.zeros((N, 8, V), np.int64)
    for q in range(N):
        for g in range(8):
            order = np.argsort(pw[q, g], kind="stable"); l = lw[q, g][order]; two = []
            for c in (0, 1):
                m = order[l == c]; i = np.searchsorted(pw[q, g][m], base[q, g], side="right"); two.append(m[np.minimum(i, len(m) - 1)])
            la[q, g] = np.where(lane[q, g] == 0, two[0], two[1]); lb[q, g] = np.where(lane[q, g] == 0, two[1], two[0])
    return jitter(rng, base), la, lb, snd
def jitter(rng, base):
    off = rng.integers(0, 2 ** 19, (1, 8, 16, 1)); size = rng.choice(np.array([1.0, 2.0, 4.0]), (N, 8, 1, 1))
    return np.clip(base[:, :, None, :] + off + np.rint(rng.standard_normal((N, 8, 16, V)) * size).astype(np.int64), 0, 2 ** 20 - 1)
def stray(rng, ptr, share):
    return np.where(rng.random(ptr.shape) < share, rng.integers(0, W, ptr.shape), ptr)
def pack(x, la, lb, snd):
    return {"x0": np.ascontiguousarray(x.reshape(N, 128, V)).astype(np.int32), "la": la.astype(np.int32), "lb": lb.astype(np.int32),
            "snd": np.stack([gtable(s.reshape(8, -1)) for s in snd])}
def setup_inputs(rng):
    x, la, lb, snd = traffic(rng)
    return pack(x, stray(rng, la, 0.1), stray(rng, lb, 0.1), snd)
def setup_inputs_ties(rng):
    snd = some(rng); x = np.zeros((N, 8, 16, V), np.int64); la = np.zeros((N, 8, V), np.int64); lb = np.zeros((N, 8, V), np.int64); h = V // 2
    for q in range(N):
        for g in range(8):
            o = rng.permutation(V); fa, fb, fo = o[0:h:2], o[1:h:2], o[h:]; n = h // 2
            xa = rng.integers(2 ** 10, 2 ** 19, (16, n)); cnt = rng.choice(np.array([0, 8, 9, 10, 16]), n)
            xb = xa + 4 + (np.argsort(rng.random((16, n)), axis=0) < cnt)
            i = rng.integers(0, n, V - h); c = rng.choice(np.array([0, 0, 7, 8, 9, 16]), V - h)
            e = np.where(c == 0, rng.integers(1, 15, (16, V - h)), (np.argsort(rng.random((16, V - h)), axis=0) >= c).astype(np.int64))
            x[q, g][:, fa] = xa; x[q, g][:, fb] = xb; x[q, g][:, fo] = xb[:, i] - e
            la[q, g] = np.arange(V); lb[q, g] = np.arange(V)
            la[q, g, fo] = stray(rng, fa[i], 0.125); lb[q, g, fo] = stray(rng, fb[i], 0.125)
    return pack(x, la, lb, snd)
def setup_inputs_weave(rng):
    snd = some(rng); base = 64 + rng.integers(0, 2 ** 15, (N, 8, V)); pw = np.concatenate([base, come(base, snd)], axis=2)
    la = np.zeros((N, 8, V), np.int64); lb = np.zeros((N, 8, V), np.int64)
    for q in range(N):
        for g in range(8):
            order = np.argsort(pw[q, g], kind="stable"); cand = order if g % 4 < 2 else order[(order < V) & (order % Q == 0)]; n = len(cand)
            la[q, g] = cand[rng.integers(0, n, V)]; hi = cand[rng.integers(2 * n // 3, n, V)]; lo = cand[rng.integers(0, n // 3, V)]
            lb[q, g] = hi if g % 2 == 0 else np.where(rng.random(V) < 0.5, hi, lo)
    return pack(jitter(rng, base), la, lb, snd)
def setup_inputs_alike(rng):
    x, la, lb, snd = traffic(rng)
    snd[:, ::2] = rng.choice(np.array([0, 3, V // 2, V - 1]), (N, 4, H, G))
    ends = np.array([0, V - 1, V, W - 1])
    la[:, 1] = rng.choice(ends, (N, V)); lb[:, 1] = rng.choice(ends, (N, V))
    la[:, 2] = rng.integers(V, W, (N, V)); lb[:, 2] = rng.integers(V, W, (N, V))
    la[:, 3] = rng.integers(0, V, (N, V)); lb[:, 3] = la[:, 3]
    lb[:, 4] = np.arange(V)
    x[:, 5] = rng.integers(0, 2 ** 20, (1, 16, 1))
    la[:, 6] = rng.choice(ends)
    return pack(x, la, lb, snd)
def setup_inputs_crowd(rng):
    snd = some(rng); x = rng.integers(0, 2 ** 20, (N, 8, 16, V)); la = rng.integers(0, W, (N, 8, V)); lb = rng.integers(0, W, (N, 8, V)); v = np.arange(V)
    for q in range(N):
        for g in range(8):
            kind = (q + g) % 4; tu = rng.permutation(v[v % Q == 0]); nt = rng.permutation(v[v % Q != 0]); xx = x[q, g]
            if kind == 0:
                hi, lo = nt[:64], nt[64:128]
                xx[:] = rng.integers(2 ** 17, 2 ** 18, (16, V)); xx[:, lo] = rng.integers(0, 2 ** 16, (16, 64)); xx[:, hi] = rng.integers(2 ** 19, 2 ** 20, (16, 64))
                la[q, g] = rng.choice(lo, V); lb[q, g] = rng.choice(hi, V)
            elif kind == 1:
                one, top = tu[0], nt[:8]
                xx[:] = rng.integers(2 ** 17, 2 ** 18, (16, V)); xx[:, nt[8:10]] = rng.integers(0, 2 ** 16, (16, 2))
                xx[:, one] = rng.integers(2 ** 19, 3 * 2 ** 18, 16); xx[:, top] = rng.integers(3 * 2 ** 18, 2 ** 20, (16, 8))
                la[q, g] = np.where(v % Q == 0, rng.choice(top, V), nt[8]); lb[q, g] = one
                la[q, g, one] = nt[9]; lb[q, g, one] = top[0]
            elif kind == 2:
                o = rng.permutation(V); n = V // 4; fa, fb, fo = o[:n], o[n:2 * n], o[2 * n:]; i = rng.integers(0, n, V - 2 * n)
                far = np.argsort(rng.random((16, 1)), axis=0) < 8
                xa = np.exp2(17 * rng.random((16, n))).astype(np.int64)
                xx[:, fa] = xa; xx[:, fb] = np.where(far, xa + rng.integers(5, 21, (16, n)), rng.integers(3 * 2 ** 18, 2 ** 20, (16, n)))
                xx[:, fo] = np.where(far, 2 ** 20 - np.exp2(18 * rng.random((16, V - 2 * n))).astype(np.int64), rng.integers(2 ** 18, 2 ** 19, (16, V - 2 * n)))
                la[q, g] = v; lb[q, g] = v; la[q, g, fo] = fa[i]; lb[q, g, fo] = fb[i]
    return pack(x, la, lb, snd)
def setup_inputs_spread(rng):
    snd = some(rng)
    x = np.minimum((np.exp2(20 * rng.random((N, 8, 1, V))) * rng.random((N, 8, 16, V))).astype(np.int64), 2 ** 20 - 1)
    end = rng.random((N, 8, 1, V)); x = np.where(end < 0.02, 0, np.where(end > 0.98, 2 ** 20 - 1, x))
    up = rng.choice(np.array([1.0, 1.5, 3.0]), (N, 8, 1)); dn = rng.choice(np.array([1.0, 1.5, 3.0]), (N, 8, 1))
    la = np.minimum((rng.random((N, 8, V)) ** up * W).astype(np.int64), W - 1); lb = W - 1 - np.minimum((rng.random((N, 8, V)) ** dn * W).astype(np.int64), W - 1)
    return pack(x, la, lb, snd)
def check_inputs(d):
    bad = []
    for k, hi in (("x0", 2 ** 20 - 1), ("la", W - 1), ("lb", W - 1), ("snd", V - 1)):
        if np.min(d[k]) < 0 or np.max(d[k]) > hi: bad.append("range of " + k)
    return bad
def reference(x0, la, lb, snd):
    x = x0.astype(np.int64).reshape(N, 8, 16, V); a = la.astype(np.int64); b = lb.astype(np.int64)
    sl = np.stack([gentries(s) for s in snd]).astype(np.int64).reshape(N, 8, H, G)
    turn = np.arange(V) % Q
    own = np.zeros((N, 8, H * G), np.int64) + np.arange(V, W)
    never = np.zeros((N, 8, H * G), bool)
    for t in range(ST):
        w = [x]
        for d in range(1, H + 1):
            q = (np.arange(N) + d) % N
            w.append(np.take_along_axis(x[q], sl[q][:, :, d - 1][:, :, None, :], 3))
        w = np.concatenate(w, axis=3)
        ga = np.take_along_axis(w, a[:, :, None, :], 3) - x; gb = np.take_along_axis(w, b[:, :, None, :], 3) - x
        gone = np.add.reduce((gb <= 0).astype(np.int64), axis=2) >= 9
        ch = (np.add.reduce((gb > ga + 4).astype(np.int64), axis=2) >= 9) & ~gone & (turn == t % Q)
        x = x + np.minimum(np.maximum(ga - 2, 0), 5)
        aw = np.concatenate([a, own], axis=2); cw = np.concatenate([ch, never], axis=2)
        aa = np.take_along_axis(aw, a, 2); ab = np.take_along_axis(aw, b, 2)
        ca = np.take_along_axis(cw, a, 2); cb = np.take_along_axis(cw, b, 2)
        na = np.where(ch | (cb & ~gone), b, np.where(ca, aa, a))
        nb = np.where(ch, a, np.where(gone | cb, ab, b))
        a, b = na, nb
    return {"yx": x.reshape(N, 128, V).astype(np.float32), "ya": a.astype(np.float32), "yb": b.astype(np.float32)}

@@ -1,0 +1,414 @@
+from concourse.mybir import AluOpType as A, ActivationFunctionType as F
+
+V, G, W, ST = 3072, 1024, 4096, 3
+XCH = 4
+GH = 2
+LAG = 4.0
+CFG = {"cc": "10 11 20 21", "xs": "", "un": "a01 a02", "va": "00 02 11 10"}
+
+SCRATCH = {
+    "xraw": ("sbuf", [128, V], "int32"),
+    "sndr": ("sbuf", [128, 64], "int32"),
+    "raw": ("sbuf", [128, 4, 96], "int32"),
+    "rawo": ("sbuf", [128, 4, 96], "float32"),
+    "w0": ("sbuf", [128, W], "float32"), "w1": ("sbuf", [128, W], "float32"), "w2": ("sbuf", [128, W], "float32"),
+    "xs1": ("sbuf", [128, V], "float32"), "xs2": ("sbuf", [128, V], "float32"),
+    "gs0": ("sbuf", [128, G], "float32"), "gs1": ("sbuf", [128, G], "float32"), "gs2": ("sbuf", [128, G], "float32"),
+    "yxs": ("sbuf", [128, V], "float32"),
+    "xa4": ("sbuf", [128, V], "float32"), "xb4": ("sbuf", [128, V], "float32"),
+    "ga": ("sbuf", [128, V], "bfloat16"), "cc": ("sbuf", [128, V], "bfloat16"),
+    "cp": ("sbuf", [128, V], "bfloat16"), "c2": ("sbuf", [128, G], "bfloat16"),
+    "tab": ("sbuf", [128, W], "bfloat16"), "rg": ("sbuf", [128, 2 * V], "bfloat16"),
+    "ones": ("sbuf", [128, 128], "bfloat16"), "di": ("sbuf", [128, 5, 128], "bfloat16"), "lagc": ("sbuf", [128, 512], "bfloat16"),
+    "i32": ("sbuf", [128, 128], "float32"), "win": ("sbuf", [128, 3, 144], "bfloat16"),
+    "t8a": ("sbuf", [128, 8], "bfloat16"), "t8b": ("sbuf", [128, 8], "bfloat16"),
+    "t8c": ("sbuf", [128, 8], "bfloat16"), "t8d": ("sbuf", [128, 8], "bfloat16"),
+    "pi": ("sbuf", [128, 64], "int32"), "pj": ("sbuf", [128, 64], "int32"),
+    "dg0": ("sbuf", [128, 4, 256], "bfloat16"), "dg1": ("sbuf", [128, 4, 256], "bfloat16"), "dg2": ("sbuf", [128, 4, 256], "bfloat16"),
+    "ch": ("sbuf", [128, 3, 256], "bfloat16"),
+    "gg": ("sbuf", [128, 192], "bfloat16"), "sg": ("sbuf", [128, 192], "bfloat16"), "thr": ("sbuf", [128, 64], "float32"),
+    "offs": ("sbuf", [128, 128], "uint16"),
+    "off0": ("sbuf", [128, 768], "uint16"), "off1": ("sbuf", [128, 768], "uint16"), "off2": ("sbuf", [128, 768], "uint16"),
+    "pf0": ("sbuf", [128, 384], "float32"), "pf1": ("sbuf", [128, 384], "float32"), "pf2": ("sbuf", [128, 384], "float32"),
+    "s1": ("sbuf", [128, 384], "float32"), "s2": ("sbuf", [128, 448], "float32"),
+    "ua": ("sbuf", [128, 448], "float32"), "ub": ("sbuf", [128, 448], "float32"), "uc": ("sbuf", [128, 448], "float32"),
+    "mi": ("sbuf", [128, 448], "int32"), "n0": ("sbuf", [128, 448], "int32"),
+    "nn": ("sbuf", [128, 384], "int32"), "lh": ("sbuf", [128, 3, 256], "int32"),
+    "px": ("psum", [128, V], "float32"), "pa": ("psum", [128, 512], "float32"), "pb": ("psum", [128, 512], "float32"),
+}
+DMAS = (["ld_snd"] + ["ld_x%d" % k for k in range(XCH)] + ["ld_p%d" % k for k in range(8)]
+        + ["td%d%d" % (t, d) for t in range(ST) for d in range(3)] + ["st_x0", "st_x1"] + ["st_p%d" % k for k in range(4)]
+        + ["xd%d%d" % (t, r) for t in (1, 2) for r in range(3)])
+SEMAPHORES = ["qv", "qs", "qt", "qg", "sent", "arr0", "arr1", "arr2"] + DMAS
+
+ORDER = """
+gh2:g ones:v tab0:v ld_x2:a ld_snd:y ld_x0:a pi:g ident:g sel1:g sel2:g gh0:g gh1:g i32:v chz:v win0:v cv22:v di4:v cv00:v ld_x1:y
+lagc:v cv21:v pj:v snd16:v sndf:v cv01:v cv20:v cv10:v cv02:v di1:v px0:t cv11:v di3:v ld_x3:a gl1:v gg00:v cv12:v cv31:v uw2:v
+px3:t px4:t ld_p6:y ld_p4:a ld_p7:a ld_p1:a ld_p0:a ld_p3:a ld_p2:a ld_p5:y sh1:v sh2:v sh0:v tr:v uw1:v gl2:v cv30:v di2:v p_m:s
+p_mi:v p_t1:v p_t2:s p_t:s gg01:v p_z:v cv32:v uw3:v p_pp:t p_n:v gl0:v lo00:v hi00:v hi02:v dg00:v lo01:v hi01:v lo02:v pq00:t
+pf00:s snd16b:v dg01:v of00:v pq01:t sd00:r sd01:r arr0:n vw16:v vw1:v dg02:v td01:y td00:y xa00:s px2:t of01:v pf01:s px5:t cp00:v
+xa01:s c20:v vp00:t pq02:t v20:t px1:t ga010:v th0:v of02:v xa02:s pr02:t ch0:v td02:y R011:s cp01:v ga000:v vp01:t G01:s ga020:v
+R021:s B01:t S01:s R010:s pr03:t cl010:v R020:s cl000:v cl020:v gg11:v sd11:r gg10:v sd10:r arr1:n ac020:t ac010:t xc010:s A01:t
+xd11:y cp02:v m101:v ac000:t C01:t vp02:t G02:s xc020:v xd12:y m201:v A02:t R001:v B02:t pf02:s lo11:v hi11:v R000:s m102:v dg11:v
+xc000:v xd10:y S02:s C02:t m202:v pq11:t of11:v A00:t lo12:v hi12:v dg12:v G00:s B00:t cp11:v pr14:t pf11:s xa11:s S00:s pq12:t
+pf12:s m100:v c21:v C00:t m200:v hi10:v lo10:v vp11:t of12:v pr15:t dg10:v th1:v ga120:v v21:t ch1:v pq10:t G11:s pf10:s cl120:v
+cp12:v ac120:t of10:v xc120:s vp12:t ga110:v ga100:v td10:y td12:y td11:y R121:s xd22:y cl110:v cl100:v gg20:v sd20:r G12:s B12:t
+R100:s S12:s ac110:t A10:t gg21:v sd21:r cp10:v R120:s A12:t C12:t m112:v ac100:t vp10:t m212:v xc100:v hi22:v lo22:v xd20:y dg22:v
+xc110:v xd21:y R111:s B11:t R110:s A11:t G10:s R101:s pq22:t S11:s of22:v m111:v pr20:t arr2:n xa22:s cp22:v C11:t pr23:t c22:v
+pf22:s B10:t ga221:v S10:s vp22:t C10:t v22:t m211:v m110:v lo21:v m210:v hi21:v lo20:v th2:v hi20:v ch2:v G22:s dg21:v dg20:v
+ga220:v pr25:t pq20:t pr21:t cl221:v of20:v cl220:v ac221:t pf20:s pq21:t xc221:s cp20:v of21:v pr22:t td22:y td20:y td21:y R201:s
+ga201:v ga210:v ga200:v cl201:v cl200:v cl210:v R220:v vp20:t pr24:t ac220:t G20:s B20:t R200:s A20:t R221:s S20:s m120:v xc220:s
+ac200:t ac210:t C20:t xc200:s xc210:s B22:t A22:t st_x0:y cp21:v ga211:v R211:s m220:v vp21:t m122:v f_r0:v f_p0:v cl211:v f_t0:v
+ac201:t S22:s G21:s C22:t m222:v ac211:t B21:t f_y0:v f_r2:v f_p2:v f_s0:v f_y2:v f_t2:v f_v00:v f_s2:v f_v01:v f_v21:v f_v20:v
+R210:s S21:s xc201:s xc211:s A21:t st_x1:y f_x0:v f_x2:v C21:t pf21:s f_o01:v m121:v m221:v f_p1:v f_o00:v f_r1:v f_y1:v f_t1:v
+f_s1:v f_v10:v f_v11:v f_o21:v f_x1:v f_o20:v f_o11:v f_o10:v st_p0:y st_p3:a st_p2:y st_p1:a
+"""
+
+
+def build(g, T, topo, core):
+    ops = []
+
+    def op(name, engs, fn, rd, wr, banks=(), cost=("e", 64)):
+        ops.append({"name": name, "engs": engs, "fn": fn, "rd": list(rd), "wr": list(wr), "banks": list(banks), "cost": cost})
+
+    rank = T.rank_of(core)
+    dst = T.cores[(rank - 1) % len(T.cores)]
+    rid, pid, _ = topo.addr(dst)
+    emask = topo.mask(core, dst)
+    w = [T.w0, T.w1, T.w2]; gs = [T.gs0, T.gs1, T.gs2]; dg = [T.dg0, T.dg1, T.dg2]; xs = [None, T.xs1, T.xs2]
+    off = [T.off0, T.off1, T.off2]; pf = [T.pf0, T.pf1, T.pf2]
+    I1, I16, I256, IM16, I16K = [T.di[:, k, :] for k in range(5)]
+
+    def dma(name, engs, out, in_, rd, wr, nbytes, rows):
+        op(name, engs, lambda q, e: q.dma_start(out, in_), rd, wr, cost=("d", nbytes, rows))
+
+    def ts(name, out, in0, s1, s2, o0, o1, rd, wr, n, banks=()):
+        if o1 is None:
+            op(name, "v", lambda q, e: q.tensor_scalar(out, in0, s1, None, o0), rd, wr, banks, ("e", n))
+        else:
+            op(name, "v", lambda q, e: q.tensor_scalar(out, in0, s1, s2, o0, o1), rd, wr, banks, ("e", n))
+
+    def tt(name, out, in0, in1, o, rd, wr, n, banks=(), kind="e"):
+        op(name, "v", lambda q, e: q.tensor_tensor(out, in0, in1, o), rd, wr, banks, (kind, n))
+
+    def cp(name, out, in_, rd, wr, n, banks=()):
+        op(name, "v", lambda q, e: q.tensor_copy(out, in_), rd, wr, banks, ("e", n))
+
+    def act(name, out, in_, func, bias, scale, rd, wr, n, banks=(), kind="e"):
+        op(name, "s", lambda q, e: q.activation(out, in_, func, bias=bias, scale=scale), rd, wr, banks, (kind, n))
+
+    def gather(name, engs, out, win, o, rd, wr, n):
+        def fn(q, e):
+            if e == "v":
+                return q.tensor_copy(out, win.indirect(o))
+            return q.activation(out, win.indirect(o), F.Copy)
+        op(name, engs, fn, rd, wr, (), ("g", n))
+
+    def mm(name, terms, rd, wr, banks, opens=True, closes=True):
+        def fn(q, e):
+            r = None
+            for k, (o, l, x, n, st) in enumerate(terms):
+                last = k == len(terms) - 1 or terms[k + 1][4]
+                r = q.matmul(o, l, x, bool(st and opens), bool(last and closes))
+            return r
+        op(name, "t", fn, rd, wr, banks, ("m", sum(x[3] for x in terms), len(terms)))
+
+    def fold(out, k, src, base):
+        return [(out, T.win[:, k, 15 - i:143 - i], src[:, base + i:base + 1024:16], 64, i == 0) for i in range(16)]
+
+    dma("ld_snd", "y", T.sndr[:], T.snd[:], [], ["sndr"], 32768, 128)
+    cw = V // XCH
+    for k in range(XCH):
+        dma("ld_x%d" % k, "ya", T.xraw[:, cw * k:cw * (k + 1)], T.x0[:, cw * k:cw * (k + 1)], [], ["xraw%d" % k], 128 * cw * 4, 128)
+    for k in range(8):
+        ab, gl, c = k // 4, (k // 2) % 2, k % 2
+        src = (T.la, T.lb)[ab]
+        dma("ld_p%d" % k, "ya", T.raw[:, 2 * ab + c, 48 * gl:48 * gl + 48], src[gl::2, 1536 * c:1536 * (c + 1)], [], ["raw%d" % k], 128 * 192, 128)
+    xr = ["xraw%d" % k for k in range(XCH)]
+
+    op("ones", "v", lambda q, e: q.memset(T.ones[:], 1.0), [], ["ones"], cost=("e", 64))
+    op("lagc", "v", lambda q, e: q.memset(T.lagc[:], LAG), [], ["lagc"], cost=("e", 256))
+    op("ident", "g", lambda q, e: q.affine_select(I1, T.ones[:], [[-1, 128]], A.is_equal, 0.0, 0, 1), ["ones"], ["di0"], cost=("p", 128))
+    for k, s in ((1, 16.0), (2, 256.0), (3, -16.0), (4, 16384.0)):
+        ts("di%d" % k, T.di[:, k, :], I1, s, None, A.mult, None, ["di0"], ["di%d" % k], 64)
+    cp("i32", T.i32[:], I1, ["di0"], ["i32"], 128)
+    op("win0", "v", lambda q, e: q.memset(T.win[:], 0.0), [], ["win0", "win1", "win2"], cost=("e", 216))
+    op("sel1", "g", lambda q, e: q.affine_select(T.t8a[:], T.ones[:, 0:8], [[-16, 8]], A.is_ge, 0.0, 0, 1), ["ones"], ["t8a"], cost=("p", 8))
+    op("sel2", "g", lambda q, e: q.affine_select(T.t8b[:], T.t8a[:], [[16, 8]], A.is_ge, 0.0, 15, -1), ["t8a"], ["t8b"], cost=("p", 8))
+    cp("vw1", T.win[:, 0, 15:128:16], T.t8b[:], ["t8b"], ["win0"], 64)
+    ts("vw16", T.win[:, 1, 15:128:16], T.t8b[:], 16.0, None, A.mult, None, ["t8b"], ["win1"], 64)
+    tt("uw1", T.t8c[:], T.di[:, 0, 0:128:16], T.di[:, 1, 1:128:16], A.add, ["di0", "di1"], ["t8c"], 64)
+    ts("uw2", T.t8d[:], T.di[:, 4, 2:128:16], 0.5, None, A.mult, None, ["di4"], ["t8d"], 64)
+    tt("uw3", T.win[:, 2, 15:128:16], T.t8c[:], T.t8d[:], A.add, ["t8c", "t8d"], ["win2"], 64)
+    op("tab0", "v", lambda q, e: q.memset(T.tab[:], 0.0), [], ["tab0", "tab1", "tab2"], cost=("e", 2048))
+    op("chz", "v", lambda q, e: q.memset(T.ch[:], 0.0), [], ["ch0", "ch1", "ch2"], cost=("e", 384))
+    op("pi", "g", lambda q, e: q.iota(T.pi[:], [[0, 64]], 0, 1), [], ["pi"], cost=("p", 64))
+    ts("pj", T.pj[:], T.pi[:], 15, None, A.bitwise_and, None, ["pi"], ["pj"], 64)
+    for t in range(ST):
+        cp("gl%d" % t, dg[t][:, 0, 192:256], T.pj[:], ["pj"], ["dgl%d" % t], 64)
+        op("gh%d" % t, "g", lambda q, e, t=t: q.iota(dg[t][:, 2, 192:256], [[1, 64]], 192, 0, allow_small_or_imprecise_dtypes=True),
+           [], ["dgh%d" % t], cost=("p", 64))
+
+    def ghosts(t):
+        n = G // GH
+        for h in range(GH):
+            nm = "%d%d" % (t, h)
+            c = slice(n * h, n * (h + 1))
+            if t == 0:
+                gather("gg" + nm, "v", gs[t][:, c], T.xraw[:, 0:V], T.offs[:, n // 16 * h:n // 16 * (h + 1)], xr + ["offs0"], ["gs" + nm], n)
+            else:
+                o = T.offs[:, 64 + n // 16 * h:64 + n // 16 * (h + 1)]
+                if nm in CFG["cc"]:
+                    tt("gg" + nm, gs[t][:, c], T.cc[:, 0:V].indirect(o), gs[t - 1][:, c], A.add,
+                       ["cc%d" % b for b in range(6)] + ["offs1", "gs%d%d" % (t - 1, h)], ["gs" + nm], n, kind="h")
+                else:
+                    gather("gg" + nm, "sv", gs[t][:, c], w[t][:, 0:V], o, ["w%d%d" % (t, r) for r in range(3)] + ["offs1"], ["gs" + nm], n)
+            op("sd" + nm, "r", lambda q, e, h=h, c=c: q.remote_dma(w[t][:, V + n * h:V + n * (h + 1)], gs[t][:, c],
+                                                                   T.sem["arr%d" % t], T.sem.sent, pid, rid, emask),
+               ["gs" + nm], ["wire" + nm], cost=("r", 128 * n * 4))
+        op("arr%d" % t, "n", None, ["wire%d%d" % (t, h) for h in range(GH)], ["wg%d" % t], cost=("n", GH * len(topo.engines(core, dst))))
+
+    cp("snd16", T.offs[:, 0:64], T.sndr[:], ["sndr"], ["offs0"], 64)
+    ghosts(0)
+    m = cw // 3
+    for k in range(XCH):
+        for r in range(3):
+            cp("cv%d%d" % (k, r), T.w0[:, G * r + m * k:G * r + m * (k + 1)], T.xraw[:, cw * k + r:cw * (k + 1):3], ["xraw%d" % k], ["w0p%d%d" % (r, k)], m)
+
+    def psum(kind, t, r):
+        if t > 0 and "%d%d" % (t - 1, r) in CFG["va"]:
+            return False
+        return (kind == "a" and r == t) or "%s%d%d" % (kind, t, r) in CFG["un"]
+
+    def base(name, t, b, lag, closes):
+        o = T.px[:, 512 * b:512 * (b + 1)]
+        src = ["w0p%d%d" % (b // 2, k) for k in range(XCH) if m * k < 512 * (b % 2 + 1) and m * (k + 1) > 512 * (b % 2)] if t == 0 else ["w%d%d" % (t, b // 2)]
+        mm(name, [(o, T.i32[:], w[t][:, 512 * b:512 * (b + 1)], 2048, True)] + ([(o, I1, T.lagc[:], 512, False)] if lag else []),
+           ["i32", "di0", "lagc"] + src, ["px%d" % b], ["X%d" % b], closes=closes)
+
+    for b in range(6):
+        if psum("a", 0, b // 2) or psum("b", 0, b // 2):
+            base("px%d" % b, 0, b, b // 2 == 0, True)
+
+    def wtok(t):
+        if t == 0:
+            return ["w0p%d%d" % (r, k) for r in range(3) for k in range(XCH)] + ["wg0"]
+        return ["w%d%d" % (t, r) for r in range(3)] + ["wg%d" % t]
+
+    def own(t, r, a, b):
+        if t == 0:
+            return T.xraw[:, 3 * a + r:3 * b:3], xr
+        return xs[t][:, G * r + a:G * r + b], ["xs%d%d" % (t, r)]
+
+    for r in range(3):
+        cp("sh%d" % r, T.s1[:, 128 * r:128 * (r + 1)], T.raw[:, :, r:96:3], ["raw%d" % k for k in range(8)], ["s1%d" % r], 128)
+    op("tr", "v", lambda q, e: q.transpose(T.s2[:, 0:384], T.s1[:]), ["s10", "s11", "s12"], ["s2a"], cost=("e", 384))
+    cp("sndf", T.s2[:, 384:448], T.sndr[:], ["sndr"], ["s2b"], 64)
+    act("p_m", T.ua[:], T.s2[:], F.Identity, -1.0 / 3.0, 1.0 / 3.0, ["s2a", "s2b"], ["ua"], 448)
+    cp("p_mi", T.mi[:], T.ua[:], ["ua"], ["mi"], 448)
+    act("p_t2", T.ub[:], T.s2[:], F.Identity, 0.0, 1024.0, ["s2a", "s2b"], ["ub"], 448)
+    act("p_t", T.uc[:, 0:384], T.s2[:, 0:384], F.Identity, -3071.5 * 8192.0, 8192.0, ["s2a"], ["uc"], 384)
+    ts("p_t1", T.ua[:], T.mi[:], -3071.0, None, A.mult, None, ["mi"], ["ua"], 448)
+    tt("p_z", T.uc[:, 0:384], T.uc[:, 0:384], T.s2[:, 0:384], A.min, ["uc", "s2a"], ["uc"], 768)
+    pk = ["pA0", "pB0", "pC0", "pA1", "pB1", "pC1"]
+    mm("p_pp", [(T.pb[:, 0:448], T.i32[:], T.ub[:], 1792, True), (T.pb[:, 0:448], T.i32[:], T.ua[:], 1792, False)], ["ua", "ub", "i32"], pk, ["PB"])
+    tt("p_n", T.n0[:, 0:384], T.pb[:, 0:384], T.uc[:, 0:384], A.max, pk + ["uc"], ["n0"], 384, ["PB"])
+    cp("snd16b", T.offs[:, 64:128], T.pb[:, 384:448], pk, ["offs1"], 64, ["PB"])
+
+    def digits(t, r, src, tok):
+        s = src[:, 128 * r:128 * (r + 1)]
+        ts("lo%d%d" % (t, r), T.lh[:, r, 0:128], s, 15, None, A.bitwise_and, None, [tok], ["lo%d" % r], 128)
+        ts("hi%d%d" % (t, r), T.lh[:, r, 128:256], s, 4, 255, A.arith_shift_right, A.bitwise_and, [tok], ["hi%d" % r], 128)
+        cp("dg%d%d" % (t, r), dg[t][:, :, 64 * r:64 * (r + 1)], T.lh[:, r, :], ["lo%d" % r, "hi%d" % r], ["dg%d%d" % (t, r)], 256)
+        d = [dg[t][:, k, 64 * r:64 * (r + 1)] for k in range(4)]
+        terms = []
+        for j in range(2):
+            o = T.pa[:, 256 + 64 * j:320 + 64 * j]
+            terms += [(o, I1, d[j], 64, True), (o, I16, d[2 + j], 64, False)]
+        for j in range(2):
+            o = T.pa[:, 384 + 64 * j:448 + 64 * j]
+            terms += [(o, I256, d[j], 64, True), (o, I1, d[2 + j], 64, False)]
+        mm("pq%d%d" % (t, r), terms, ["dg%d%d" % (t, r), "di0", "di1", "di2"], ["pq"], ["PA"])
+        cp("of%d%d" % (t, r), off[t][:, 256 * r:256 * (r + 1)], T.pa[:, 256:512], ["pq"], ["of%d%d" % (t, r)], 256, ["PA"])
+        act("pf%d%d" % (t, r), pf[t][:, 128 * r:128 * (r + 1)], T.pa[:, 256:384], F.Identity, 4096.0, 1.0, ["pq"], ["pf%d%d" % (t, r)], 128, ["PA"])
+
+    for r in range(3):
+        digits(0, r, T.n0, "n0")
+
+    slot = [0]
+    for t in range(ST):
+        wt, wk, last = w[t], wtok(t), t == ST - 1
+        win = wt[:, 0:W]
+        dgt = ["dg%d%d" % (t, r) for r in range(3)]
+        dma("td%d0" % t, "y", T.tab[0:128:16, :], dg[t][:, 0, :], dgt + ["dgl%d" % t], ["tab0"], 65536, 128)
+        dma("td%d1" % t, "y", T.tab[1:128:16, :], dg[t][:, 2, :], dgt + ["dgh%d" % t], ["tab1"], 65536, 128)
+
+        def oa(r, a=0, b=64): return off[t][:, 256 * r + a:256 * r + b]
+        def ob(r): return off[t][:, 256 * r + 64:256 * r + 128]
+        cl = [(t + j) % 3 for j in range(3)]
+        for r in cl:
+            c = slice(G * r, G * (r + 1))
+            lag = LAG if r == t else 0.0
+            if r == t or psum("a", t, r):
+                act("xa%d%d" % (t, r), T.xa4[:, c], win.indirect(oa(r)), F.Identity, lag, 1.0, wk + ["of%d%d" % (t, r)], ["xa%d" % r], G, kind="g")
+            if psum("b", t, r):
+                act("xb%d%d" % (t, r), T.xb4[:, c], win.indirect(ob(r)), F.Identity, lag, 1.0, wk + ["of%d%d" % (t, r)], ["xb%d" % r], G, kind="g")
+                tt("cp%d%d" % (t, r), T.cp[:, c], T.xb4[:, c], T.px[:, c], A.is_le, ["xb%d" % r, "px%d" % (2 * r), "px%d" % (2 * r + 1)], ["cp%d" % r], G,
+                   ["X%d" % (2 * r), "X%d" % (2 * r + 1)])
+            else:
+                x, xk = own(t, r, 0, G)
+                tt("cp%d%d" % (t, r), T.cp[:, c], win.indirect(ob(r)), x, A.is_le, wk + xk + ["of%d%d" % (t, r)], ["cp%d" % r], G, kind="h")
+            mm("vp%d%d" % (t, r), fold(T.pa[:, 64 * r:64 * (r + 1)], 1, T.cp, G * r), ["cp%d" % r, "win1"], ["cnt%d" % r], ["PA"])
+            if r == t:
+                tt("c2%d" % t, T.c2[:], win.indirect(ob(r)), T.xa4[:, c], A.is_gt, wk + ["of%d%d" % (t, r), "xa%d" % r], ["c2"], G, kind="h")
+                mm("v2%d" % t, fold(T.pa[:, 192:256], 0, T.c2, 0), ["c2", "win0"], ["cnt2"], ["PA"])
+                ts("th%d" % t, T.thr[:], T.pa[:, 64 * r:64 * (r + 1)], -127.0, 8.5, A.add, A.max, ["cnt%d" % r], ["thr"], 64, ["PA"])
+                tt("ch%d" % t, T.ch[:, t, 64 * r:64 * (r + 1)], T.pa[:, 192:256], T.thr[:], A.is_gt, ["cnt2", "thr"], ["ch%d" % t], 64, ["PA"])
+                dma("td%d2" % t, "y", T.tab[2:128:16, :], T.ch[:, t, :], ["ch%d" % t], ["tab2"], 65536, 128)
+            act("G%d%d" % (t, r), T.gg[:, 64 * r:64 * (r + 1)], T.pa[:, 64 * r:64 * (r + 1)], F.Relu, -65536.0, 512.0, ["cnt%d" % r], ["G%d" % r], 64, ["PA"])
+        pieces = 2 if last else 1
+        n = G // pieces
+        for h in range(pieces):
+            for r in cl:
+                lo, hi = G * r + n * h, G * r + n * (h + 1)
+                bs = [2 * r + h] if last else [2 * r, 2 * r + 1]
+                nm = "%d%d%d" % (t, r, h)
+                gk = ["ga%d" % b for b in bs]; ck = ["cc%d" % b for b in bs]; pk = ["px%d" % b for b in bs]; xb = ["X%d" % b for b in bs]
+                if psum("a", t, r):
+                    tt("ga" + nm, T.ga[:, lo:hi], T.xa4[:, lo:hi], T.px[:, lo:hi], A.subtract, ["xa%d" % r] + pk, gk, n, xb)
+                else:
+                    x, xk = own(t, r, n * h, n * (h + 1))
+                    tt("ga" + nm, T.ga[:, lo:hi], win.indirect(oa(r, n // 16 * h, n // 16 * (h + 1))), x, A.subtract,
+                       wk + xk + ["of%d%d" % (t, r)], gk, n, kind="h")
+                ts("cl" + nm, T.cc[:, lo:hi], T.ga[:, lo:hi], 2.0, 7.0, A.max, A.min, gk, ck, n // 2)
+                va = "%d%d" % (t, r) in CFG["va"]
+                if not va:
+                    for b in bs:
+                        base("pr%d%d" % (t, b), t, b, r == t + 1, False)
+                mm("ac" + nm, [(T.px[:, 512 * b:512 * (b + 1)], I1, T.cc[:, 512 * b:512 * (b + 1)], 512, True) for b in bs],
+                   ck + pk + ["di0"], pk, xb, opens=va)
+                if last:
+                    act("xc" + nm, T.yxs[:, 1536 * h + r:1536 * (h + 1):3], T.px[:, lo:hi], F.Identity, -2.0 * ST, 1.0, pk, ["yx%d%d" % (h, r)], n, xb)
+                else:
+                    k = "%d%d" % (t + 1, r)
+                    lag = -LAG if r == t + 1 else 0.0
+                    if va:
+                        tt("xc" + nm, w[t + 1][:, lo:hi], T.px[:, lo:hi], wt[:, lo:hi], A.add, pk + wk[:-1], ["w" + k], n, xb)
+                    else:
+                        act("xc" + nm, w[t + 1][:, lo:hi], T.px[:, lo:hi], F.Identity, lag, 1.0, pk, ["w" + k], n, xb)
+                    if psum("a", t + 1, r) and psum("b", t + 1, r):
+                        pass
+                    elif k in CFG["xs"] and not va:
+                        act("xd" + k, xs[t + 1][:, lo:hi], T.px[:, lo:hi], F.Identity, lag, 1.0, pk, ["xs" + k], n, xb)
+                    else:
+                        dma("xd" + k, "y", xs[t + 1][:, lo:hi], w[t + 1][:, lo:hi], ["w" + k], ["xs" + k], 128 * G * 4, 128)
+            if last:
+                dma("st_x%d" % h, "y", T.yx[:, 1536 * h:1536 * (h + 1)], T.yxs[:, 1536 * h:1536 * (h + 1)], ["yx%d%d" % (h, r) for r in range(3)], [], 128 * 1536 * 4, 128)
+        if not last:
+            ghosts(t + 1)
+        for r in [(t + 1 + j) % 3 for j in range(3)]:
+            nm = "%d%d" % (t, r)
+            for j in range(2):
+                gather("R%s%d" % (nm, j), "sv", T.rg[:, G * (2 * r + j):G * (2 * r + j + 1)], T.tab[:, 0:W], off[t][:, 256 * r + 128 + 64 * j:256 * r + 192 + 64 * j],
+                       ["tab0", "tab1", "tab2", "of" + nm], ["R%d%d" % (r, j)], G)
+            s = slot[0]; slot[0] = 1 - s
+            b0 = 256 * s
+            pA, pB, pC, pD = [T.pb[:, b0 + 64 * k:b0 + 64 * (k + 1)] for k in range(4)]
+            gr = T.gg[:, 64 * r:64 * (r + 1)]
+            sv = T.sg[:, 64 * r:64 * (r + 1)]
+            d = [dg[t][:, k, 64 * r:64 * (r + 1)] for k in range(4)]
+            chv = T.ch[:, t, 64 * r:64 * (r + 1)]
+            mm("A" + nm, fold(pA, 2, T.rg, G * 2 * r), ["R%d0" % r, "win2"], ["pA%d" % s], ["PB"])
+            mm("B" + nm, fold(pB, 2, T.rg, G * (2 * r + 1)) + [(pB, I1, gr, 64, False)], ["R%d1" % r, "win2", "G%d" % r, "di0"], ["pB%d" % s], ["PB"])
+            act("S" + nm, sv, pB, F.Sign, -8191.5, 1.0, ["pB%d" % s], ["sg%d" % r], 64, ["PB"])
+            tc = [(pC, I16K, sv, 64, True), (pC, I1, d[1], 64, False), (pC, I16, d[3], 64, False), (pC, IM16, gr, 64, False)]
+            rd = ["sg%d" % r, "G%d" % r, "dg" + nm, "di0", "di1", "di3", "di4"]
+            if r == t:
+                tc += [(pC, I16K, chv, 64, False), (pC, I16K, chv, 64, False),
+                       (pD, I1, d[0], 64, True), (pD, I16, d[2], 64, False), (pD, IM16, gr, 64, False), (pD, I16K, chv, 64, False)]
+                rd += ["ch%d" % t]
+            mm("C" + nm, tc, rd, ["pC%d" % s], ["PB"])
+            k2 = 128 if r == t else 64
+            nv = T.nn[:, 128 * r:128 * (r + 1)]
+            tt("m1" + nm, nv, T.pb[:, b0:b0 + 128], pf[t][:, 128 * r:128 * (r + 1)], A.max, ["pA%d" % s, "pB%d" % s, "pf" + nm], ["nn%d" % r], 128, ["PB"])
+            tt("m2" + nm, T.nn[:, 128 * r:128 * r + k2], T.pb[:, b0 + 128:b0 + 128 + k2], T.nn[:, 128 * r:128 * r + k2], A.max, ["pC%d" % s, "nn%d" % r], ["nn%d" % r], k2, ["PB"])
+            if not last:
+                digits(t + 1, r, T.nn, "nn%d" % r)
+            else:
+                c = slice(128 * r, 128 * (r + 1))
+                ts("f_p%d" % r, T.lh[:, r, 0:128], nv, 4095, None, A.bitwise_and, None, ["nn%d" % r], ["lo%d" % r], 128)
+                ts("f_r%d" % r, T.lh[:, r, 128:256], nv, 10, 3, A.arith_shift_right, A.bitwise_and, ["nn%d" % r], ["hi%d" % r], 128)
+                ts("f_y%d" % r, T.ua[:, c], T.lh[:, r, 0:128], 3071.0, 2.0, A.min, A.mult, ["lo%d" % r, "ua"], ["fa%d" % r], 128)
+                ts("f_t%d" % r, T.ub[:, c], T.lh[:, r, 128:256], 2.0, -3071.0, A.min, A.mult, ["hi%d" % r, "ub"], ["fb%d" % r], 128)
+                tt("f_s%d" % r, T.ua[:, c], T.ua[:, c], T.lh[:, r, 0:128], A.add, ["fa%d" % r, "lo%d" % r], ["fa%d" % r], 256)
+                for u in range(2):
+                    cu = slice(128 * r + u, 128 * (r + 1), 2)
+                    tt("f_v%d%d" % (r, u), T.s1[:, 128 * r + 64 * u:128 * r + 64 * (u + 1)], T.ub[:, cu], T.ua[:, cu], A.add,
+                       ["fa%d" % r, "fb%d" % r, "s2a"], ["fv%d%d" % (r, u)], 128)
+                op("f_x%d" % r, "v", lambda q, e, c=c: q.transpose(T.uc[:, c], T.s1[:, c]), ["fv%d0" % r, "fv%d1" % r, "uc"], ["fc%d" % r], cost=("e", 128))
+                for u in range(2):
+                    cp("f_o%d%d" % (r, u), T.rawo[:, :, 48 * u + r:48 * (u + 1):3], T.uc[:, 128 * r + 64 * u:128 * r + 64 * (u + 1)], ["fc%d" % r], ["ro%d%d" % (r, u)], 64)
+    for k in range(4):
+        dma("st_p%d" % k, "ya", (T.ya, T.yb)[k // 2][k % 2::2, :], T.rawo[:, k, :], ["ro%d%d" % (r, u) for r in range(3) for u in range(2)], [], 128 * 384, 128)
+    return ops
+
+
+QUEUE = {"v": "v", "s": "s", "a": "s", "t": "t", "y": "y", "g": "g", "r": "g"}
+
+
+def depend(seq):
+    wrote, read, bank, deps = {}, {}, {}, []
+    for k, (o, e) in enumerate(seq):
+        d = set()
+        for x in o["rd"]:
+            if x in wrote: d.add(wrote[x])
+        for x in o["wr"]:
+            if x in wrote: d.add(wrote[x])
+            d.update(read.get(x, []))
+        for b in o["banks"]:
+            d.update(j for q, j in bank.setdefault(b, {}).items() if q != e)
+            bank[b][e] = k
+        for x in o["rd"]:
+            read.setdefault(x, []).append(k)
+        for x in o["wr"]:
+            wrote[x] = k; read[x] = []
+        d.discard(k)
+        deps.append(sorted(d))
+    return deps
+
+
+def rank_program(g, core, T, topo):
+    if T.rank_of(core) is None:
+        return
+    ops = build(g, T, topo, core)
+    byname = {o["name"]: o for o in ops}
+    seq = [(byname[x[:-2]], x[-1]) for x in ORDER.split()]
+    assert len(seq) == len(ops) == len(byname)
+    deps = depend(seq)
+    qs = {"v": g.vector, "s": g.scalar, "t": g.tensor, "y": g.sync, "g": g}
+    needed = set(j for k, d in enumerate(deps) if seq[k][1] != "n" for j in d)
+    done, count, waited, sent = {}, {"v": 0, "s": 0, "t": 0, "g": 0}, {}, 0
+    for k, (o, e) in enumerate(seq):
+        if e == "n":
+            done[k] = (o["name"], o["cost"][1])
+            continue
+        qn = QUEUE[e]
+        need = {}
+        for j in deps[k]:
+            s, v = done[j]
+            need[s] = max(need.get(s, 0), v)
+        for s, v in need.items():
+            if waited.get((qn, s), 0) < v:
+                qs[qn].wait_ge(T.sem[s], v); waited[(qn, s)] = v
+        ins = o["fn"](qs[qn], e)
+        if e == "r":
+            sent += len(topo.engines(core, T.cores[(T.rank_of(core) - 1) % len(T.cores)]))
+        elif e in "ya":
+            ins.then_inc(T.sem[o["name"]], 16); done[k] = (o["name"], 16)
+        elif k in needed:
+            count[e] += 1
+            ins.then_inc(T.sem["q" + e], 1); done[k] = ("q" + e, count[e])
+    g.wait_ge(T.sem.sent, sent)
+    for k, (o, e) in enumerate(seq):
+        if e in "ya" and k not in needed:
+            g.wait_ge(T.sem[o["name"]], 16)

@@ -1,373 +1,469 @@
+import math
+from concourse.bass import DstId, RemoteDMATransfer
 from concourse.mybir import AluOpType as A, ActivationFunctionType as F
 
 V, G, W, ST = 3072, 1024, 4096, 3
+CS = 88
+FL, LOW = 88.0, -96.0
 XCH = 4
 GH = 2
-LAG = 4.0
-CFG = {"cc": "10 11 20 21", "xs": "", "un": "a01 a02", "va": "00 02 11 10"}
+HA = (2, 2, 2)
+ADD = ("vvvvvv", "vvvvvv", "d")
+GT = True
+SB = ("", "", "")
+GS = "ss"
+XT = ("ss", "ss")
+RV = ("", "", "21")
+TURNS, SWAPS, HEAT, SEED = 3, 200000, 150.0, 7
+FOLD, ACC = 0.3, 1.5
+AD = (0, 3, 5, 6)
+XH = (1, 1)
+G0 = (0, 256, 1024)
+MA = ("", "", "")
+EST = []
+LISTS = [["cp.T c2# ga.T0 ch# E1# ga.N0 ga.O0 cp.N ga.N1 ga.T1 ga.O1 cp.O",
+          "cp.T c2# ga.T0 ch# E1# ga.T1 ga.N0 ga.N1 cp.N ga.O0 ga.O1 cp.O",
+          "cp.T c2# ga.T0 ch# E1# ga.T1 cp.N ga.N0 ga.O0 ga.N1 ga.O1 cp.O"],
+         ["xa.T R.N1 R.N0 R.O1 R.O0", "xa.T -R.T1 -R.T0 R.N0 R.N1 R.O1 R.O0", "xa.T -R.T1 -R.T0 R.N0 R.N1 R.O1 R.O0 R.T0"]]
 
 SCRATCH = {
-    "xraw": ("sbuf", [128, V], "int32"),
-    "sndr": ("sbuf", [128, 64], "int32"),
-    "raw": ("sbuf", [128, 4, 96], "int32"),
-    "rawo": ("sbuf", [128, 4, 96], "float32"),
+    "xraw": ("sbuf", [128, V], "int32"), "sndr": ("sbuf", [128, 64], "int32"),
+    "raw": ("sbuf", [128, 4, 96], "int32"), "rawo": ("sbuf", [128, 4, 96], "float32"),
     "w0": ("sbuf", [128, W], "float32"), "w1": ("sbuf", [128, W], "float32"), "w2": ("sbuf", [128, W], "float32"),
-    "xs1": ("sbuf", [128, V], "float32"), "xs2": ("sbuf", [128, V], "float32"),
+    "xs1": ("sbuf", [128, V], "float32"), "xs2": ("sbuf", [128, V], "float32"), "yxs": ("sbuf", [128, V], "float32"),
     "gs0": ("sbuf", [128, G], "float32"), "gs1": ("sbuf", [128, G], "float32"), "gs2": ("sbuf", [128, G], "float32"),
-    "yxs": ("sbuf", [128, V], "float32"),
-    "xa4": ("sbuf", [128, V], "float32"), "xb4": ("sbuf", [128, V], "float32"),
-    "ga": ("sbuf", [128, V], "bfloat16"), "cc": ("sbuf", [128, V], "bfloat16"),
-    "cp": ("sbuf", [128, V], "bfloat16"), "c2": ("sbuf", [128, G], "bfloat16"),
-    "tab": ("sbuf", [128, W], "bfloat16"), "rg": ("sbuf", [128, 2 * V], "bfloat16"),
-    "ones": ("sbuf", [128, 128], "bfloat16"), "di": ("sbuf", [128, 5, 128], "bfloat16"), "lagc": ("sbuf", [128, 512], "bfloat16"),
-    "i32": ("sbuf", [128, 128], "float32"), "win": ("sbuf", [128, 3, 144], "bfloat16"),
-    "t8a": ("sbuf", [128, 8], "bfloat16"), "t8b": ("sbuf", [128, 8], "bfloat16"),
-    "t8c": ("sbuf", [128, 8], "bfloat16"), "t8d": ("sbuf", [128, 8], "bfloat16"),
-    "pi": ("sbuf", [128, 64], "int32"), "pj": ("sbuf", [128, 64], "int32"),
-    "dg0": ("sbuf", [128, 4, 256], "bfloat16"), "dg1": ("sbuf", [128, 4, 256], "bfloat16"), "dg2": ("sbuf", [128, 4, 256], "bfloat16"),
-    "ch": ("sbuf", [128, 3, 256], "bfloat16"),
-    "gg": ("sbuf", [128, 192], "bfloat16"), "sg": ("sbuf", [128, 192], "bfloat16"), "thr": ("sbuf", [128, 64], "float32"),
-    "offs": ("sbuf", [128, 128], "uint16"),
+    "gsm": ("sbuf", [128, G], "float32"), "xa4": ("sbuf", [128, G], "float32"), "xb": ("sbuf", [128, G], "float32"), "xt": ("sbuf", [128, G], "float32"),
+    "ga": ("sbuf", [128, V], "bfloat16"), "cp": ("sbuf", [128, V], "bfloat16"), "c2": ("sbuf", [128, G], "bfloat16"),
+    "cc0": ("sbuf", [128, V], "bfloat16"), "cc1": ("sbuf", [128, V], "bfloat16"), "cc2": ("sbuf", [128, V], "bfloat16"),
+    "tab": ("sbuf", [128, 48 * CS], "bfloat16"), "tae": ("sbuf", [128, 48 * CS], "bfloat16"), "rg": ("sbuf", [128, 2 * V], "bfloat16"),
+    "ones": ("sbuf", [128, 512], "bfloat16"),
+    "k49": ("sbuf", [128, 64], "bfloat16"), "wf": ("sbuf", [128, 2, 2, 128], "bfloat16"),
+    "di": ("sbuf", [128, 13, 128], "bfloat16"), "i32": ("sbuf", [128, 2, 128], "float32"),
+    "win": ("sbuf", [128, 3, 144], "bfloat16"), "wm": ("sbuf", [128, 4, 128], "bfloat16"),
+    "dq": ("sbuf", [128, 2, 128], "bfloat16"), "dv": ("sbuf", [128, 2, 128], "float32"),
+    "t8a": ("sbuf", [128, 8], "bfloat16"), "t8b": ("sbuf", [128, 8], "bfloat16"), "t8c": ("sbuf", [128, 8], "bfloat16"),
+    "pi": ("sbuf", [128, 1], "int32"), "pj": ("sbuf", [128, 2], "int32"), "col": ("sbuf", [128, 2], "float32"),
+    "sd": ("sbuf", [128, 2, 3, CS], "bfloat16"), "tc": ("sbuf", [128, 2, 3, CS], "bfloat16"),
+    "da": ("sbuf", [128, 2, 3, CS], "bfloat16"), "db": ("sbuf", [128, 3, 128], "bfloat16"),
+    "e0": ("sbuf", [128, 2, 3, CS], "bfloat16"), "e1": ("sbuf", [128, 2, 3, CS], "bfloat16"), "e2": ("sbuf", [128, 2, 3, CS], "bfloat16"),
+    "h0": ("sbuf", [128, 2, 3, CS], "bfloat16"), "h1": ("sbuf", [128, 2, 3, CS], "bfloat16"), "h2": ("sbuf", [128, 2, 3, CS], "bfloat16"),
+    "sw": ("sbuf", [128, 128], "bfloat16"), "gt": ("sbuf", [128, 3, 128], "bfloat16"), "sg": ("sbuf", [128, 3, 256], "bfloat16"),
+    "xm": ("sbuf", [128, 3, 256], "bfloat16"), "cq": ("sbuf", [128, 3, 128], "bfloat16"),
+    "s1": ("sbuf", [128, 3, 128], "float32"), "s2": ("sbuf", [128, 3, 128], "float32"), "vs": ("sbuf", [128, 3, 128], "float32"),
+    "offs": ("sbuf", [128, 64], "uint16"),
     "off0": ("sbuf", [128, 768], "uint16"), "off1": ("sbuf", [128, 768], "uint16"), "off2": ("sbuf", [128, 768], "uint16"),
-    "pf0": ("sbuf", [128, 384], "float32"), "pf1": ("sbuf", [128, 384], "float32"), "pf2": ("sbuf", [128, 384], "float32"),
-    "s1": ("sbuf", [128, 384], "float32"), "s2": ("sbuf", [128, 448], "float32"),
-    "ua": ("sbuf", [128, 448], "float32"), "ub": ("sbuf", [128, 448], "float32"), "uc": ("sbuf", [128, 448], "float32"),
-    "mi": ("sbuf", [128, 448], "int32"), "n0": ("sbuf", [128, 448], "int32"),
-    "nn": ("sbuf", [128, 384], "int32"), "lh": ("sbuf", [128, 3, 256], "int32"),
-    "px": ("psum", [128, V], "float32"), "pa": ("psum", [128, 512], "float32"), "pb": ("psum", [128, 512], "float32"),
+    "px": ("psum", [128, 2048], "float32"), "pc": ("psum", [128, 512], "float32"), "py": ("psum", [128, 512], "float32"),
+    "pp": ("psum", [128, 512], "float32"), "pf": ("psum", [128, 512], "float32"),
 }
-DMAS = (["ld_snd"] + ["ld_x%d" % k for k in range(XCH)] + ["ld_p%d" % k for k in range(8)]
-        + ["td%d%d" % (t, d) for t in range(ST) for d in range(3)] + ["st_x0", "st_x1"] + ["st_p%d" % k for k in range(4)]
-        + ["xd%d%d" % (t, r) for t in (1, 2) for r in range(3)])
-SEMAPHORES = ["qv", "qs", "qt", "qg", "sent", "arr0", "arr1", "arr2"] + DMAS
-
-ORDER = """
-gh2:g ones:v tab0:v ld_x2:a ld_snd:y ld_x0:a pi:g ident:g sel1:g sel2:g gh0:g gh1:g i32:v chz:v win0:v cv22:v di4:v cv00:v ld_x1:y
-lagc:v cv21:v pj:v snd16:v sndf:v cv01:v cv20:v cv10:v cv02:v di1:v px0:t cv11:v di3:v ld_x3:a gl1:v gg00:v cv12:v cv31:v uw2:v
-px3:t px4:t ld_p6:y ld_p4:a ld_p7:a ld_p1:a ld_p0:a ld_p3:a ld_p2:a ld_p5:y sh1:v sh2:v sh0:v tr:v uw1:v gl2:v cv30:v di2:v p_m:s
-p_mi:v p_t1:v p_t2:s p_t:s gg01:v p_z:v cv32:v uw3:v p_pp:t p_n:v gl0:v lo00:v hi00:v hi02:v dg00:v lo01:v hi01:v lo02:v pq00:t
-pf00:s snd16b:v dg01:v of00:v pq01:t sd00:r sd01:r arr0:n vw16:v vw1:v dg02:v td01:y td00:y xa00:s px2:t of01:v pf01:s px5:t cp00:v
-xa01:s c20:v vp00:t pq02:t v20:t px1:t ga010:v th0:v of02:v xa02:s pr02:t ch0:v td02:y R011:s cp01:v ga000:v vp01:t G01:s ga020:v
-R021:s B01:t S01:s R010:s pr03:t cl010:v R020:s cl000:v cl020:v gg11:v sd11:r gg10:v sd10:r arr1:n ac020:t ac010:t xc010:s A01:t
-xd11:y cp02:v m101:v ac000:t C01:t vp02:t G02:s xc020:v xd12:y m201:v A02:t R001:v B02:t pf02:s lo11:v hi11:v R000:s m102:v dg11:v
-xc000:v xd10:y S02:s C02:t m202:v pq11:t of11:v A00:t lo12:v hi12:v dg12:v G00:s B00:t cp11:v pr14:t pf11:s xa11:s S00:s pq12:t
-pf12:s m100:v c21:v C00:t m200:v hi10:v lo10:v vp11:t of12:v pr15:t dg10:v th1:v ga120:v v21:t ch1:v pq10:t G11:s pf10:s cl120:v
-cp12:v ac120:t of10:v xc120:s vp12:t ga110:v ga100:v td10:y td12:y td11:y R121:s xd22:y cl110:v cl100:v gg20:v sd20:r G12:s B12:t
-R100:s S12:s ac110:t A10:t gg21:v sd21:r cp10:v R120:s A12:t C12:t m112:v ac100:t vp10:t m212:v xc100:v hi22:v lo22:v xd20:y dg22:v
-xc110:v xd21:y R111:s B11:t R110:s A11:t G10:s R101:s pq22:t S11:s of22:v m111:v pr20:t arr2:n xa22:s cp22:v C11:t pr23:t c22:v
-pf22:s B10:t ga221:v S10:s vp22:t C10:t v22:t m211:v m110:v lo21:v m210:v hi21:v lo20:v th2:v hi20:v ch2:v G22:s dg21:v dg20:v
-ga220:v pr25:t pq20:t pr21:t cl221:v of20:v cl220:v ac221:t pf20:s pq21:t xc221:s cp20:v of21:v pr22:t td22:y td20:y td21:y R201:s
-ga201:v ga210:v ga200:v cl201:v cl200:v cl210:v R220:v vp20:t pr24:t ac220:t G20:s B20:t R200:s A20:t R221:s S20:s m120:v xc220:s
-ac200:t ac210:t C20:t xc200:s xc210:s B22:t A22:t st_x0:y cp21:v ga211:v R211:s m220:v vp21:t m122:v f_r0:v f_p0:v cl211:v f_t0:v
-ac201:t S22:s G21:s C22:t m222:v ac211:t B21:t f_y0:v f_r2:v f_p2:v f_s0:v f_y2:v f_t2:v f_v00:v f_s2:v f_v01:v f_v21:v f_v20:v
-R210:s S21:s xc201:s xc211:s A21:t st_x1:y f_x0:v f_x2:v C21:t pf21:s f_o01:v m121:v m221:v f_p1:v f_o00:v f_r1:v f_y1:v f_t1:v
-f_s1:v f_v10:v f_v11:v f_o21:v f_x1:v f_o20:v f_o11:v f_o10:v st_p0:y st_p3:a st_p2:y st_p1:a
-"""
+DMAS = (["ld_snd", "sdc"] + ["ld_x%d" % k for k in range(XCH)] + ["ld_p%d" % k for k in range(4)]
+        + ["td%d%d" % (t, d) for t in range(ST) for d in range(5)] + ["st_p%d" % k for k in range(4)]
+        + ["xd%d%d" % (t, k) for t in (1, 2) for k in range(6)] + ["st_x%d" % k for k in range(6)] + ["ad%d" % k for k in range(6)])
+SEMAPHORES = ["qv", "qs", "qt", "qg", "sent", "arr0", "arr1", "arr2", "iss1", "iss2"] + DMAS
 
 
-def build(g, T, topo, core):
+def build(T, topo, core):
     ops = []
 
-    def op(name, engs, fn, rd, wr, banks=(), cost=("e", 64)):
-        ops.append({"name": name, "engs": engs, "fn": fn, "rd": list(rd), "wr": list(wr), "banks": list(banks), "cost": cost})
+    def op(name, eng, fn, rd, wr, banks=(), cost=64.0):
+        ops.append({"name": name, "eng": eng, "fn": fn, "rd": list(rd), "wr": list(wr), "banks": list(banks), "cost": cost})
 
-    rank = T.rank_of(core)
-    dst = T.cores[(rank - 1) % len(T.cores)]
+    dst = T.cores[(T.rank_of(core) - 1) % len(T.cores)]
     rid, pid, _ = topo.addr(dst)
     emask = topo.mask(core, dst)
-    w = [T.w0, T.w1, T.w2]; gs = [T.gs0, T.gs1, T.gs2]; dg = [T.dg0, T.dg1, T.dg2]; xs = [None, T.xs1, T.xs2]
-    off = [T.off0, T.off1, T.off2]; pf = [T.pf0, T.pf1, T.pf2]
-    I1, I16, I256, IM16, I16K = [T.di[:, k, :] for k in range(5)]
+    w = [T.w0, T.w1, T.w2]; gs = [T.gs0, T.gs1, T.gs2]; xs = [T.xraw, T.xs1, T.xs2]; cc = [T.cc0, T.cc1, T.cc2]
+    off = [T.off0, T.off1, T.off2]; et = [T.e0, T.e1, T.e2]; ht = [T.h0, T.h1, T.h2]
+    SC = (1.0, -1.0, FL, -FL, FL / 2, -48.0, -2.0 * ST, -FL / 2, -2 * FL, 4.0 - 2 * ST, 4.0, -FL - LOW, -1.5 * FL - LOW)
+    I1, IM1, IF, IMF, IH, IM48, IM6, IMH, IM2F, IM2, I4, IKA, IKB = [T.di[:, k, :] for k in range(13)]
+    GA = 1.56
 
-    def dma(name, engs, out, in_, rd, wr, nbytes, rows):
-        op(name, engs, lambda q, e: q.dma_start(out, in_), rd, wr, cost=("d", nbytes, rows))
+    def dma(name, eng, out, in_, rd, wr, nbytes, rows=128):
+        op(name, eng, lambda q: q.dma_start(out, in_), rd, wr, cost=(nbytes, rows))
 
     def ts(name, out, in0, s1, s2, o0, o1, rd, wr, n, banks=()):
         if o1 is None:
-            op(name, "v", lambda q, e: q.tensor_scalar(out, in0, s1, None, o0), rd, wr, banks, ("e", n))
+            op(name, "v", lambda q: q.tensor_scalar(out, in0, s1, None, o0), rd, wr, banks, n)
         else:
-            op(name, "v", lambda q, e: q.tensor_scalar(out, in0, s1, s2, o0, o1), rd, wr, banks, ("e", n))
+            op(name, "v", lambda q: q.tensor_scalar(out, in0, s1, s2, o0, o1), rd, wr, banks, n)
 
-    def tt(name, out, in0, in1, o, rd, wr, n, banks=(), kind="e"):
-        op(name, "v", lambda q, e: q.tensor_tensor(out, in0, in1, o), rd, wr, banks, (kind, n))
+    def tt(name, out, in0, in1, o, rd, wr, n, banks=()):
+        op(name, "v", lambda q: q.tensor_tensor(out, in0, in1, o), rd, wr, banks, n)
 
     def cp(name, out, in_, rd, wr, n, banks=()):
-        op(name, "v", lambda q, e: q.tensor_copy(out, in_), rd, wr, banks, ("e", n))
+        op(name, "v", lambda q: q.tensor_copy(out, in_), rd, wr, banks, n)
 
-    def act(name, out, in_, func, bias, scale, rd, wr, n, banks=(), kind="e"):
-        op(name, "s", lambda q, e: q.activation(out, in_, func, bias=bias, scale=scale), rd, wr, banks, (kind, n))
+    def act(name, out, in_, func, bias, scale, rd, wr, n, banks=()):
+        op(name, "s", lambda q: q.activation(out, in_, func, bias=bias, scale=scale), rd, wr, banks, n)
 
-    def gather(name, engs, out, win, o, rd, wr, n):
-        def fn(q, e):
-            if e == "v":
-                return q.tensor_copy(out, win.indirect(o))
-            return q.activation(out, win.indirect(o), F.Copy)
-        op(name, engs, fn, rd, wr, (), ("g", n))
+    def sel(name, out, in_, pat, cmp, fill, base, cm, rd, wr, n):
+        op(name, "g", lambda q: q.affine_select(out, in_, pat, cmp, fill, base, cm), rd, wr, cost=200 + 2 * n)
+
+    def iota(name, out, pat, base, cm, rd, wr, n):
+        op(name, "g", lambda q: q.iota(out, pat, base, cm, allow_small_or_imprecise_dtypes=True), rd, wr, cost=160 + 2 * n)
 
     def mm(name, terms, rd, wr, banks, opens=True, closes=True):
-        def fn(q, e):
+        def fn(q):
             r = None
             for k, (o, l, x, n, st) in enumerate(terms):
                 last = k == len(terms) - 1 or terms[k + 1][4]
                 r = q.matmul(o, l, x, bool(st and opens), bool(last and closes))
             return r
-        op(name, "t", fn, rd, wr, banks, ("m", sum(x[3] for x in terms), len(terms)))
+        op(name, "t", fn, rd, wr, banks, sum(x[3] + 16 for x in terms) / 2)
 
-    def fold(out, k, src, base):
-        return [(out, T.win[:, k, 15 - i:143 - i], src[:, base + i:base + 1024:16], 64, i == 0) for i in range(16)]
+    def fold(buf, c0, k, src, base, more=(), own=True):
+        terms = []
+        for b in range(2):
+            o = buf[:, c0 + 64 * b:c0 + 64 * (b + 1)]
+            terms += [(o, T.win[:, k, 14 - 2 * m:142 - 2 * m], src[:, base + 2 * m + b:base + G:16], 64, own and m == 0) for m in range(8)]
+            terms += [(o, l, x(b), 64, False) for l, x in more]
+        return terms
 
-    dma("ld_snd", "y", T.sndr[:], T.snd[:], [], ["sndr"], 32768, 128)
+    def half(buf, r):
+        return lambda b: buf[:, r, 64 * b:64 * (b + 1)]
+
+    def seg(buf, r):
+        return lambda b: buf[:, b, r, 0:64]
+
     cw = V // XCH
+    dma("ld_snd", "y", T.sndr[:], T.snd[:], [], ["sndr"], 32768)
     for k in range(XCH):
-        dma("ld_x%d" % k, "ya", T.xraw[:, cw * k:cw * (k + 1)], T.x0[:, cw * k:cw * (k + 1)], [], ["xraw%d" % k], 128 * cw * 4, 128)
-    for k in range(8):
-        ab, gl, c = k // 4, (k // 2) % 2, k % 2
-        src = (T.la, T.lb)[ab]
-        dma("ld_p%d" % k, "ya", T.raw[:, 2 * ab + c, 48 * gl:48 * gl + 48], src[gl::2, 1536 * c:1536 * (c + 1)], [], ["raw%d" % k], 128 * 192, 128)
-    xr = ["xraw%d" % k for k in range(XCH)]
+        dma("ld_x%d" % k, "ay"[k % 2], T.xraw[:, cw * k:cw * (k + 1)], T.x0[:, cw * k:cw * (k + 1)], [], ["xr%d" % k], 128 * cw * 4)
+    for k in range(4):
+        dma("ld_p%d" % k, "ay"[k % 2], T.raw[:, k, :], (T.la, T.lb)[k // 2][k % 2::2, :], [], ["raw%d" % k], 128 * 384)
+    xr = ["xr%d" % k for k in range(XCH)]
 
-    op("ones", "v", lambda q, e: q.memset(T.ones[:], 1.0), [], ["ones"], cost=("e", 64))
-    op("lagc", "v", lambda q, e: q.memset(T.lagc[:], LAG), [], ["lagc"], cost=("e", 256))
-    op("ident", "g", lambda q, e: q.affine_select(I1, T.ones[:], [[-1, 128]], A.is_equal, 0.0, 0, 1), ["ones"], ["di0"], cost=("p", 128))
-    for k, s in ((1, 16.0), (2, 256.0), (3, -16.0), (4, 16384.0)):
-        ts("di%d" % k, T.di[:, k, :], I1, s, None, A.mult, None, ["di0"], ["di%d" % k], 64)
-    cp("i32", T.i32[:], I1, ["di0"], ["i32"], 128)
-    op("win0", "v", lambda q, e: q.memset(T.win[:], 0.0), [], ["win0", "win1", "win2"], cost=("e", 216))
-    op("sel1", "g", lambda q, e: q.affine_select(T.t8a[:], T.ones[:, 0:8], [[-16, 8]], A.is_ge, 0.0, 0, 1), ["ones"], ["t8a"], cost=("p", 8))
-    op("sel2", "g", lambda q, e: q.affine_select(T.t8b[:], T.t8a[:], [[16, 8]], A.is_ge, 0.0, 15, -1), ["t8a"], ["t8b"], cost=("p", 8))
-    cp("vw1", T.win[:, 0, 15:128:16], T.t8b[:], ["t8b"], ["win0"], 64)
-    ts("vw16", T.win[:, 1, 15:128:16], T.t8b[:], 16.0, None, A.mult, None, ["t8b"], ["win1"], 64)
-    tt("uw1", T.t8c[:], T.di[:, 0, 0:128:16], T.di[:, 1, 1:128:16], A.add, ["di0", "di1"], ["t8c"], 64)
-    ts("uw2", T.t8d[:], T.di[:, 4, 2:128:16], 0.5, None, A.mult, None, ["di4"], ["t8d"], 64)
-    tt("uw3", T.win[:, 2, 15:128:16], T.t8c[:], T.t8d[:], A.add, ["t8c", "t8d"], ["win2"], 64)
-    op("tab0", "v", lambda q, e: q.memset(T.tab[:], 0.0), [], ["tab0", "tab1", "tab2"], cost=("e", 2048))
-    op("chz", "v", lambda q, e: q.memset(T.ch[:], 0.0), [], ["ch0", "ch1", "ch2"], cost=("e", 384))
-    op("pi", "g", lambda q, e: q.iota(T.pi[:], [[0, 64]], 0, 1), [], ["pi"], cost=("p", 64))
-    ts("pj", T.pj[:], T.pi[:], 15, None, A.bitwise_and, None, ["pi"], ["pj"], 64)
-    for t in range(ST):
-        cp("gl%d" % t, dg[t][:, 0, 192:256], T.pj[:], ["pj"], ["dgl%d" % t], 64)
-        op("gh%d" % t, "g", lambda q, e, t=t: q.iota(dg[t][:, 2, 192:256], [[1, 64]], 192, 0, allow_small_or_imprecise_dtypes=True),
-           [], ["dgh%d" % t], cost=("p", 64))
+    op("ones", "v", lambda q: q.memset(T.ones[:], 1.0), [], ["ones"], cost=256)
+    op("tae0", "v", lambda q: q.memset(T.tae[:], 0.0), [], ["tab2", "tab3"], cost=24 * CS)
+    act("tab0", T.tab[:], T.tae[:], F.Identity, 0.0, 1.0, ["tab2", "tab3"], ["tab0", "tab1", "tab4"], 48 * CS)
+    op("win0", "v", lambda q: q.memset(T.win[:], 0.0), [], ["win"], cost=216)
+    op("wm0", "v", lambda q: q.memset(T.wm[:], 0.0), [], ["wm%d" % k for k in range(4)], cost=256)
+    op("dv0", "v", lambda q: q.memset(T.dv[:], 0.0), [], ["dv0", "dv1"], cost=256)
+    sel("di0", I1, T.ones[:, 0:128], [[-1, 128]], A.is_equal, 0.0, 0, 1, ["ones"], ["di0"], 128)
+    op("k49", "v", lambda q: q.memset(T.k49[:], 49.0), [], ["k49"])
+    for k in range(1, 13):
+        act("di%d" % k, T.di[:, k, :], I1, F.Identity, 0.0, SC[k], ["di0"], ["di%d" % k], 128)
+    for k in range(2):
+        act("i32%d" % k, T.i32[:, k, :], I1, F.Identity, 0.0, SC[k], ["di0"], ["i32%d" % k], 128)
+    sel("t8a", T.t8a[:], T.ones[:, 0:8], [[-16, 8]], A.is_ge, 0.0, 0, 1, ["ones"], ["t8a"], 8)
+    sel("t8b", T.t8b[:], T.t8a[:], [[16, 8]], A.is_ge, 0.0, 15, -1, ["t8a"], ["t8b"], 8)
+    act("t8c", T.t8c[:], T.di[:, 2, 4:128:16], F.Identity, 0.0, 2.0, ["di2"], ["t8c"], 64)
+    for e in range(2):
+        act("win0%d" % e, T.win[:, 0, 14 + e:128:16], T.t8b[:], F.Identity, 0.0, 1.0, ["t8b", "win"], ["win0%d" % e], 64)
+        act("win1%d" % e, T.win[:, 1, 14 + e:128:16], T.di[:, 0, 2 + e:128:16], F.Identity, 0.0, 1.0, ["di0", "win"], ["win1%d" % e], 64)
+        tt("win2%d" % e, T.win[:, 2, 14 + e:128:16], T.di[:, 0, e:128:16], T.t8c[:], A.add, ["di0", "t8c", "win"], ["win2%d" % e], 64)
+    wk_ = [["win%d%d" % (k, e) for e in range(2)] for k in range(3)]
+    for k, ws in enumerate(((48.0, 1.0), (1.0, float(CS)))):
+        for b in range(2):
+            o = T.wm[:, 2 * k + b, b:128:2]
+            for e in range(2):
+                sel("wm%d%d%d" % (k, b, e), o, o, [[-2, 64]], A.not_equal, ws[e], -e, 1, ["wm%d" % (2 * k + b)], ["wm%d" % (2 * k + b)], 64)
+    for k in range(2):
+        act("wf%d" % k, T.wf[:, k], T.wm[:, 0:2, :], F.Identity, 0.0, (FL / 2, -FL / 2)[k], ["wm0", "wm1"], ["wf%d" % k], 256)
+    for b in range(2):
+        for e in range(2):
+            act("dq%d%d" % (b, e), T.dq[:, b, e:128:2], T.di[:, (0, 5)[e], b:128:2], F.Identity, 0.0, 1.0, ["di0", "di5"], ["dq%d%d" % (b, e)], 64)
+        act("dv%d" % (b + 1), T.dv[:, b, 1:128:2], T.di[:, 0, b:128:2], F.Identity, 0.0, 1.0, ["di0", "dv%d" % b], ["dw%d" % b], 64)
+    op("pi", "g", lambda q: q.iota(T.pi[:], [[0, 1]], 0, 1), [], ["pi"], cost=170)
+    ts("pj0", T.pj[:, 0:1], T.pi[:], 1, None, A.bitwise_and, None, ["pi"], ["pj0"], 64)
+    ts("pj1", T.pj[:, 1:2], T.pi[:], 14, None, A.bitwise_and, None, ["pi"], ["pj1"], 64)
+    ts("col0", T.col[:, 0:1], T.pj[:, 0:1], 49.0 * 129.0, LOW - 129.0, A.mult, A.add, ["pj0"], ["col0"], 64)
+    ts("col1", T.col[:, 1:2], T.pj[:, 1:2], 3.0, LOW, A.mult, A.add, ["pj1"], ["col1"], 64)
+    iota("tc", T.tc[:], [[0, 6], [1, CS]], int(LOW), 0, [], ["tc"], 6 * CS)
+    iota("sd0", T.sd[:], [[1, 6], [0, CS]], 0, 0, [], ["sd"], 6 * CS)
+    act("sd1", T.sd[:], T.sd[:], F.Identity, T.col[:, 1:2], 1.0, ["sd", "col1"], ["sd"], 6 * CS)
+    dma("sdc", "y", T.sd[0:128:2], T.tc[0:128:2], ["tc", "sd"], ["sd"], 64 * 12 * CS, 64)
+    act("dag", T.da[:, :, :, 64:CS], T.sd[:, :, :, 64:CS], F.Identity, 0.0, 1.0, ["sd"], ["dag"], 6 * (CS - 64))
 
-    def ghosts(t):
-        n = G // GH
-        for h in range(GH):
-            nm = "%d%d" % (t, h)
-            c = slice(n * h, n * (h + 1))
-            if t == 0:
-                gather("gg" + nm, "v", gs[t][:, c], T.xraw[:, 0:V], T.offs[:, n // 16 * h:n // 16 * (h + 1)], xr + ["offs0"], ["gs" + nm], n)
-            else:
-                o = T.offs[:, 64 + n // 16 * h:64 + n // 16 * (h + 1)]
-                if nm in CFG["cc"]:
-                    tt("gg" + nm, gs[t][:, c], T.cc[:, 0:V].indirect(o), gs[t - 1][:, c], A.add,
-                       ["cc%d" % b for b in range(6)] + ["offs1", "gs%d%d" % (t - 1, h)], ["gs" + nm], n, kind="h")
-                else:
-                    gather("gg" + nm, "sv", gs[t][:, c], w[t][:, 0:V], o, ["w%d%d" % (t, r) for r in range(3)] + ["offs1"], ["gs" + nm], n)
-            op("sd" + nm, "r", lambda q, e, h=h, c=c: q.remote_dma(w[t][:, V + n * h:V + n * (h + 1)], gs[t][:, c],
-                                                                   T.sem["arr%d" % t], T.sem.sent, pid, rid, emask),
-               ["gs" + nm], ["wire" + nm], cost=("r", 128 * n * 4))
-        op("arr%d" % t, "n", None, ["wire%d%d" % (t, h) for h in range(GH)], ["wg%d" % t], cost=("n", GH * len(topo.engines(core, dst))))
+    def cck(t, ks):
+        return sorted(set("cc%d%d%d" % (t, r, k * HA[t] // 6) for r in range(3) for k in ks))
 
-    cp("snd16", T.offs[:, 0:64], T.sndr[:], ["sndr"], ["offs0"], 64)
-    ghosts(0)
-    m = cw // 3
-    for k in range(XCH):
-        for r in range(3):
-            cp("cv%d%d" % (k, r), T.w0[:, G * r + m * k:G * r + m * (k + 1)], T.xraw[:, cw * k + r:cw * (k + 1):3], ["xraw%d" % k], ["w0p%d%d" % (r, k)], m)
+    def cover(lo, hi, t):
+        n = cw if t == 0 else 512
+        return range(lo // n, (hi + n - 1) // n)
 
-    def psum(kind, t, r):
-        if t > 0 and "%d%d" % (t - 1, r) in CFG["va"]:
-            return False
-        return (kind == "a" and r == t) or "%s%d%d" % (kind, t, r) in CFG["un"]
+    def wtok(t, lo=0, hi=V):
+        return ["w%d_%d" % (t, k) for k in cover(lo, hi, t)]
 
-    def base(name, t, b, lag, closes):
-        o = T.px[:, 512 * b:512 * (b + 1)]
-        src = ["w0p%d%d" % (b // 2, k) for k in range(XCH) if m * k < 512 * (b % 2 + 1) and m * (k + 1) > 512 * (b % 2)] if t == 0 else ["w%d%d" % (t, b // 2)]
-        mm(name, [(o, T.i32[:], w[t][:, 512 * b:512 * (b + 1)], 2048, True)] + ([(o, I1, T.lagc[:], 512, False)] if lag else []),
-           ["i32", "di0", "lagc"] + src, ["px%d" % b], ["X%d" % b], closes=closes)
-
-    for b in range(6):
-        if psum("a", 0, b // 2) or psum("b", 0, b // 2):
-            base("px%d" % b, 0, b, b // 2 == 0, True)
-
-    def wtok(t):
-        if t == 0:
-            return ["w0p%d%d" % (r, k) for r in range(3) for k in range(XCH)] + ["wg0"]
-        return ["w%d%d" % (t, r) for r in range(3)] + ["wg%d" % t]
+    def xtok(t, lo=0, hi=V):
+        return [("xr%d" % k if t == 0 else "xs%d_%d" % (t, k)) for k in cover(lo, hi, t)]
 
     def own(t, r, a, b):
-        if t == 0:
-            return T.xraw[:, 3 * a + r:3 * b:3], xr
-        return xs[t][:, G * r + a:G * r + b], ["xs%d%d" % (t, r)]
+        if t and r == t and XT[t - 1]:
+            return T.xt[:, a:b], ["xt%d" % h for h in range(a // 512, (b + 511) // 512)]
+        return xs[t][:, 3 * a + r:3 * b:3], xtok(t, 3 * a, 3 * b)
 
-    for r in range(3):
-        cp("sh%d" % r, T.s1[:, 128 * r:128 * (r + 1)], T.raw[:, :, r:96:3], ["raw%d" % k for k in range(8)], ["s1%d" % r], 128)
-    op("tr", "v", lambda q, e: q.transpose(T.s2[:, 0:384], T.s1[:]), ["s10", "s11", "s12"], ["s2a"], cost=("e", 384))
-    cp("sndf", T.s2[:, 384:448], T.sndr[:], ["sndr"], ["s2b"], 64)
-    act("p_m", T.ua[:], T.s2[:], F.Identity, -1.0 / 3.0, 1.0 / 3.0, ["s2a", "s2b"], ["ua"], 448)
-    cp("p_mi", T.mi[:], T.ua[:], ["ua"], ["mi"], 448)
-    act("p_t2", T.ub[:], T.s2[:], F.Identity, 0.0, 1024.0, ["s2a", "s2b"], ["ub"], 448)
-    act("p_t", T.uc[:, 0:384], T.s2[:, 0:384], F.Identity, -3071.5 * 8192.0, 8192.0, ["s2a"], ["uc"], 384)
-    ts("p_t1", T.ua[:], T.mi[:], -3071.0, None, A.mult, None, ["mi"], ["ua"], 448)
-    tt("p_z", T.uc[:, 0:384], T.uc[:, 0:384], T.s2[:, 0:384], A.min, ["uc", "s2a"], ["uc"], 768)
-    pk = ["pA0", "pB0", "pC0", "pA1", "pB1", "pC1"]
-    mm("p_pp", [(T.pb[:, 0:448], T.i32[:], T.ub[:], 1792, True), (T.pb[:, 0:448], T.i32[:], T.ua[:], 1792, False)], ["ua", "ub", "i32"], pk, ["PB"])
-    tt("p_n", T.n0[:, 0:384], T.pb[:, 0:384], T.uc[:, 0:384], A.max, pk + ["uc"], ["n0"], 384, ["PB"])
-    cp("snd16b", T.offs[:, 64:128], T.pb[:, 384:448], pk, ["offs1"], 64, ["PB"])
+    def grow(t, nm, who, c, out, toks, tok, keep=None):
+        b = nextbank() if keep is None else keep
+        o = T.px[:, 512 * b:512 * (b + 1)]
+        if who == "s":
+            lag = [] if keep is None else [(o, (IM2, I4)[t], T.ones[:], 512, False)]
+            mm("pr" + nm, [(o, T.i32[:, 0, :], w[t][:, c], 2048, True)] + lag, ["i320", "ones", "di9", "di10"] + wtok(t, c.start, c.stop), ["px%d" % b], ["X%d" % b], closes=False)
+            mm("ac" + nm, [(o, I1, cc[t][:, c], 512, True)], toks + ["px%d" % b, "di0"], ["px%d" % b], ["X%d" % b], opens=False)
+            act("xc" + nm, out, o, F.Identity, -4.0 if lag else -2.0 * ST if t == 0 else 0.0, 1.0, ["px%d" % b], tok, 512, ["X%d" % b])
+        else:
+            mm("ac" + nm, ([(o, IM6, T.ones[:], 512, True)] if t == 0 else []) + [(o, I1, cc[t][:, c], 512, t > 0)],
+               toks + ["di0", "di6", "ones"], ["px%d" % b], ["X%d" % b])
+            tt("xc" + nm, out, o, w[t][:, c], A.add, ["px%d" % b] + wtok(t, c.start, c.stop), tok, 512, ["X%d" % b])
 
-    def digits(t, r, src, tok):
-        s = src[:, 128 * r:128 * (r + 1)]
-        ts("lo%d%d" % (t, r), T.lh[:, r, 0:128], s, 15, None, A.bitwise_and, None, [tok], ["lo%d" % r], 128)
-        ts("hi%d%d" % (t, r), T.lh[:, r, 128:256], s, 4, 255, A.arith_shift_right, A.bitwise_and, [tok], ["hi%d" % r], 128)
-        cp("dg%d%d" % (t, r), dg[t][:, :, 64 * r:64 * (r + 1)], T.lh[:, r, :], ["lo%d" % r, "hi%d" % r], ["dg%d%d" % (t, r)], 256)
-        d = [dg[t][:, k, 64 * r:64 * (r + 1)] for k in range(4)]
-        terms = []
-        for j in range(2):
-            o = T.pa[:, 256 + 64 * j:320 + 64 * j]
-            terms += [(o, I1, d[j], 64, True), (o, I16, d[2 + j], 64, False)]
-        for j in range(2):
-            o = T.pa[:, 384 + 64 * j:448 + 64 * j]
-            terms += [(o, I256, d[j], 64, True), (o, I1, d[2 + j], 64, False)]
-        mm("pq%d%d" % (t, r), terms, ["dg%d%d" % (t, r), "di0", "di1", "di2"], ["pq"], ["PA"])
-        cp("of%d%d" % (t, r), off[t][:, 256 * r:256 * (r + 1)], T.pa[:, 256:512], ["pq"], ["of%d%d" % (t, r)], 256, ["PA"])
-        act("pf%d%d" % (t, r), pf[t][:, 128 * r:128 * (r + 1)], T.pa[:, 256:384], F.Identity, 4096.0, 1.0, ["pq"], ["pf%d%d" % (t, r)], 128, ["PA"])
+    def ghosts(t):
+        for h in range(GH):
+            nm = "%d%d" % (t, h)
+            c = slice(G0[h], G0[h + 1]) if t == 0 else slice(G // GH * h, G // GH * (h + 1))
+            n = c.stop - c.start
+            o = T.offs[:, c.start // 16:c.stop // 16]
+            land = w[t][:, V + c.start:V + c.stop]
+            if t == 0:
+                cp("gg" + nm, gs[0][:, c], T.xraw[:, 0:V].indirect(o), xr + ["offs"], ["gs" + nm], GA * n)
+                if GS != "ww" and h == GH - 1:
+                    act("gm", T.gsm[:], gs[0][:], F.Identity, -2.0 * ST, 1.0, ["gs0%d" % k for k in range(GH)], ["gm%d" % k for k in range(GH)], G)
+            elif GS[t - 1] == "w":
+                act("gg" + nm, gs[t][:, c], w[t][:, 0:V].indirect(o), F.Copy, 0.0, 1.0, wtok(t) + ["offs"], ["gs" + nm], GA * n)
+            elif GS[t - 1] == "s":
+                act("gg" + nm, gs[t][:, c], cc[t - 1][:, 0:V].indirect(o), F.Copy, 0.0, 1.0, cck(t - 1, range(6)) + ["offs"], ["gs" + nm], GA * n)
+                srcs = [T.gsm[:, c]] + [gs[k][:, c] for k in range(1, t + 1)]
+                op("sd" + nm, "r", lambda q, land=land, srcs=srcs: q.remote_dma_fused([RemoteDMATransfer(
+                    dst_ids=[DstId(rid=rid, pnc=pid)], dma_engine_mask=emask, remote_sem=T.sem["arr%d" % t], srcs=srcs,
+                    dsts=[land], alu_op=1)], local_sem=T.sem.sent),
+                   ["gm%d" % h] + ["gs%d%d" % (k, h) for k in range(1, t + 1)], ["wire" + nm], cost=(128 * n * 4 * (1 + FOLD * t), 128))
+                continue
+            else:
+                prev, tok = (T.gsm, "gm%d" % h) if t == 1 else (gs[t - 1], "gs%d%d" % (t - 1, h))
+                tt("gg" + nm, gs[t][:, c], cc[t - 1][:, 0:V].indirect(o), prev[:, c], A.add, cck(t - 1, range(6)) + ["offs", tok], ["gs" + nm], GA * n)
+            op("sd" + nm, "r", lambda q, land=land, c=c: q.remote_dma(land, gs[t][:, c], T.sem["arr%d" % t], T.sem.sent, pid, rid, emask),
+               ["gs" + nm], ["wire" + nm], cost=(128 * n * 4, 128))
+        if t:
+            op("iss%d" % t, "i", None, ["wire%d%d" % (t, h) for h in range(GH)], ["iss%d" % t])
+        op("arr%d" % t, "n", None, ["wire%d%d" % (t, h) for h in range(GH)], ["wg%d" % t], cost=GH * len(topo.engines(core, dst)))
 
-    for r in range(3):
-        digits(0, r, T.n0, "n0")
-
-    slot = [0]
+    cp("snd16", T.offs[:], T.sndr[:], ["sndr"], ["offs"], 64)
+    ghosts(0)
     for t in range(ST):
-        wt, wk, last = w[t], wtok(t), t == ST - 1
-        win = wt[:, 0:W]
-        dgt = ["dg%d%d" % (t, r) for r in range(3)]
-        dma("td%d0" % t, "y", T.tab[0:128:16, :], dg[t][:, 0, :], dgt + ["dgl%d" % t], ["tab0"], 65536, 128)
-        dma("td%d1" % t, "y", T.tab[1:128:16, :], dg[t][:, 2, :], dgt + ["dgh%d" % t], ["tab1"], 65536, 128)
+        for nm, buf in (("e", et[t]), ("h", ht[t])):
+            if t == 0:
+                op("z%s0" % nm, "v", lambda q, buf=buf: q.memset(buf[:], 0.0), [], [nm + "0"], cost=3 * CS)
+            else:
+                iota("z%s%d" % (nm, t), buf[:], [[0, 6 * CS]], 0, 0, ["wire0%d" % (GH - 1)], ["%s%d" % (nm, t)], 6 * CS)
+    for k in range(XCH):
+        cp("cv%d" % k, T.w0[:, cw * k:cw * (k + 1)], T.xraw[:, cw * k:cw * (k + 1)], ["xr%d" % k], ["w0_%d" % k], cw)
 
-        def oa(r, a=0, b=64): return off[t][:, 256 * r + a:256 * r + b]
-        def ob(r): return off[t][:, 256 * r + 64:256 * r + 128]
+    for r in range(3):
+        for u in range(2):
+            cp("sh%d%d" % (r, u), T.s1[:, r, 64 * u:64 * (u + 1)], T.raw[:, :, 48 * u + r:48 * (u + 1):3], ["raw%d" % k for k in range(4)], ["s1%d%d" % (r, u)], 64)
+        op("tr%d" % r, "v", lambda q, r=r: q.transpose(T.s2[:, r, :], T.s1[:, r, :]), ["s1%d0" % r, "s1%d1" % r], ["s2%d" % r], cost=128)
+    for u in range(2):
+        act("vs%d" % u, T.vs[:, :, u:128:2], T.s2[:, :, 64 * u:64 * (u + 1)], F.Identity, 0.0, 1.0, ["s20", "s21", "s22"], ["vs%d" % u], 192)
+    act("cq", T.cq[:], T.vs[:], F.Identity, 129.0 - 23.5 / 48.0, 1.0 / 48.0, ["vs0", "vs1"], ["cq"], 384)
+    for r in range(3):
+        cp("ov0%d" % r, off[0][:, 256 * r:256 * r + 128], T.vs[:, r, :], ["vs0", "vs1"], ["ov0%d" % r], 128)
+        terms = []
+        pd, pk, bk = ((T.pp, ["P"], "PP"), (T.py, ["Q0", "Q1"], "PY"), (T.pc, ["cnt0", "cnt1"], "PC"))[r]
+        for j in range(2):
+            for b in range(2):
+                o = pd[:, 128 * j + 64 * b:128 * j + 64 * (b + 1)]
+                terms += [(o, T.dq[:, b, :], T.cq[:, r, 64 * j:64 * (j + 1)], 64, True), (o, T.dv[:, b, :], T.vs[:, r, 64 * j:64 * (j + 1)], 256, False)]
+        mm("dg0%d" % r, terms, ["cq", "vs0", "vs1", "dq00", "dq01", "dq10", "dq11", "dw0", "dw1"], pk, [bk])
+        act("da0%d" % r, T.da[:, :, r, 0:64], pd[:, 0:128], F.Identity, T.col[:, 0:1], 1.0, pk + ["col0"], ["da%d" % r], 128, [bk])
+        act("db0%d" % r, T.db[:, r, :], pd[:, 128:256], F.Identity, T.col[:, 0:1], 1.0, pk + ["col0"], ["db%d" % r], 128, [bk])
+    if GT:
+        for h in range(2):
+            o = T.px[:, 512 * (2 + h):512 * (3 + h)]
+            mm("po%d" % h, [(o, T.i32[:, 0, :], T.w0[:, 1536 * h:1536 * (h + 1):3], 2048, True), (o, I4, T.ones[:], 512, False)],
+               ["i320", "ones", "di10"] + wtok(0, 1536 * h, 1536 * (h + 1)), ["px%d" % (2 + h)], ["X%d" % (2 + h)])
+
+    def offsets(t, r):
+        for k in (1,) if t == 0 else (0, 1):
+            nm = "%s%d%d" % ("vu"[k], t, r)
+            terms = []
+            for j, x in enumerate((seg(T.da, r), half(T.db, r))):
+                o = T.pf[:, 256 + 128 * k + 64 * j:320 + 128 * k + 64 * j]
+                terms += [(o, T.wm[:, 2 * k + b, :], x(b), 64, b == 0) for b in range(2)]
+            mm("p" + nm, terms, ["da%d" % r, "db%d" % r, "wm%d" % (2 * k), "wm%d" % (2 * k + 1)], ["pq%d" % k], ["PF"])
+            ts("o" + nm, off[t][:, 256 * r + 128 * k:256 * r + 128 * (k + 1)], T.pf[:, 256 + 128 * k:384 + 128 * k], -LOW * (49, CS + 1)[k], None, A.add, None,
+               ["pq%d" % k], ["o" + nm], 128, ["PF"])
+
+    for r in range(3):
+        offsets(0, r)
+
+    bank = [0]
+
+    def nextbank():
+        bank[0] = (bank[0] + 1) % (2 if GT else 4)
+        return bank[0]
+
+    for t in range(ST):
+        last = t == ST - 1
+        win = w[t][:, 0:W]
+        wk = wtok(t) + ["wg%d" % t]
+        for e in range(2):
+            dma("td%d%d" % (t, e), "y", T.tab[e:128:16, :], T.da[e:128:2], ["da0", "da1", "da2", "dag"], ["tab%d" % e], 768 * CS, 64)
+
+        def lst(r, k, a=0, b=64): return off[t][:, 256 * r + 64 * k + a:256 * r + 64 * k + b]
         cl = [(t + j) % 3 for j in range(3)]
         for r in cl:
+            nm = "%d%d" % (t, r)
             c = slice(G * r, G * (r + 1))
-            lag = LAG if r == t else 0.0
-            if r == t or psum("a", t, r):
-                act("xa%d%d" % (t, r), T.xa4[:, c], win.indirect(oa(r)), F.Identity, lag, 1.0, wk + ["of%d%d" % (t, r)], ["xa%d" % r], G, kind="g")
-            if psum("b", t, r):
-                act("xb%d%d" % (t, r), T.xb4[:, c], win.indirect(ob(r)), F.Identity, lag, 1.0, wk + ["of%d%d" % (t, r)], ["xb%d" % r], G, kind="g")
-                tt("cp%d%d" % (t, r), T.cp[:, c], T.xb4[:, c], T.px[:, c], A.is_le, ["xb%d" % r, "px%d" % (2 * r), "px%d" % (2 * r + 1)], ["cp%d" % r], G,
-                   ["X%d" % (2 * r), "X%d" % (2 * r + 1)])
+            thr = -8.5
+            if r == t:
+                act("xa" + nm, T.xa4[:], win.indirect(lst(r, 0)), F.Identity, 4.0, 1.0, wk + ["ov" + nm], ["xa4"], GA * G)
+            if str(r) in SB[t]:
+                act("xb" + nm, T.xb[:], win.indirect(lst(r, 1)), F.Identity, 0.0, 1.0, wk + ["ov" + nm], ["xb"], GA * G)
+                for h in range(2):
+                    b = nextbank()
+                    o = T.px[:, 512 * b:512 * (b + 1)]
+                    mm("pb%s%d" % (nm, h), [(o, T.i32[:, 1, :], w[t][:, 1536 * h + r:1536 * (h + 1):3], 2048, True)], ["i321"] + wtok(t), ["px%d" % b], ["X%d" % b], closes=False)
+                    mm("pc%s%d" % (nm, h), [(o, T.i32[:, 0, :], T.xb[:, 512 * h:512 * (h + 1)], 2048, True)], ["xb", "i320", "px%d" % b], ["px%d" % b], ["X%d" % b], opens=False)
+                    act("cp%s%d" % (nm, h), T.cp[:, G * r + 512 * h:G * r + 512 * (h + 1)], o, F.Sign, 0.5, -1.0, ["px%d" % b], ["cp%d%d" % (r, h)], 512, ["X%d" % b])
+                thr = -1.0
             else:
                 x, xk = own(t, r, 0, G)
-                tt("cp%d%d" % (t, r), T.cp[:, c], win.indirect(ob(r)), x, A.is_le, wk + xk + ["of%d%d" % (t, r)], ["cp%d" % r], G, kind="h")
-            mm("vp%d%d" % (t, r), fold(T.pa[:, 64 * r:64 * (r + 1)], 1, T.cp, G * r), ["cp%d" % r, "win1"], ["cnt%d" % r], ["PA"])
+                tt("cp" + nm, T.cp[:, c], win.indirect(lst(r, 1)), x, A.is_le, wk + xk + ["ov" + nm], ["cp%d0" % r, "cp%d1" % r], GA * G)
+            mm("vp" + nm, fold(T.pc, 128 * r, 0, T.cp, G * r), ["cp%d0" % r, "cp%d1" % r] + wk_[0], ["cnt%d" % r], ["PC"])
+            act("G" + nm, T.gt[:, r, :], T.pc[:, 128 * r:128 * (r + 1)], F.Sign, thr, 1.0, ["cnt%d" % r], ["G%d" % r], 128, ["PC"])
             if r == t:
-                tt("c2%d" % t, T.c2[:], win.indirect(ob(r)), T.xa4[:, c], A.is_gt, wk + ["of%d%d" % (t, r), "xa%d" % r], ["c2"], G, kind="h")
-                mm("v2%d" % t, fold(T.pa[:, 192:256], 0, T.c2, 0), ["c2", "win0"], ["cnt2"], ["PA"])
-                ts("th%d" % t, T.thr[:], T.pa[:, 64 * r:64 * (r + 1)], -127.0, 8.5, A.add, A.max, ["cnt%d" % r], ["thr"], 64, ["PA"])
-                tt("ch%d" % t, T.ch[:, t, 64 * r:64 * (r + 1)], T.pa[:, 192:256], T.thr[:], A.is_gt, ["cnt2", "thr"], ["ch%d" % t], 64, ["PA"])
-                dma("td%d2" % t, "y", T.tab[2:128:16, :], T.ch[:, t, :], ["ch%d" % t], ["tab2"], 65536, 128)
-            act("G%d%d" % (t, r), T.gg[:, 64 * r:64 * (r + 1)], T.pa[:, 64 * r:64 * (r + 1)], F.Relu, -65536.0, 512.0, ["cnt%d" % r], ["G%d" % r], 64, ["PA"])
-        pieces = 2 if last else 1
-        n = G // pieces
-        for h in range(pieces):
+                tt("c2%d" % t, T.c2[:], win.indirect(lst(r, 1)), T.xa4[:], A.is_gt, wk + ["ov" + nm, "xa4"], ["c2"], GA * G)
+                terms = []
+                d = nextbank() if t else None
+                pd, dk, db_ = (T.px, ["px%d" % d], "X%d" % d) if t else (T.pp, ["P"], "PP")
+                d0 = 512 * d if t else 0
+                for k, x in enumerate((seg(T.sd, r), half(T.db, r))):
+                    for b in range(2):
+                        o = pd[:, d0 + 128 * k + 64 * b:d0 + 128 * k + 64 * (b + 1)]
+                        terms += [(o, I1, seg(T.da, r)(b), 64, True), (o, IM1, x(b), 64, False)]
+                mm("D%d" % t, terms, ["da%d" % r, "db%d" % r, "sd", "di0", "di1"], dk, [db_])
+                mm("v2%d" % t, fold(T.pc, 384, 0, T.c2, 0, [(IM48, half(T.gt, r))]), ["c2", "G%d" % r, "di5"] + wk_[0], ["cnt2"], ["PC"])
+                chv = ht[t][:, :, r, 0:64]
+                ts("ch%d" % t, chv, T.pc[:, 384:512], 56.5, None, A.is_gt, None, ["cnt2"], ["h%d" % t], 128, ["PC"])
+                tt("E1%d" % t, et[t][:, :, r, 0:64], pd[:, d0:d0 + 128], chv, A.mult, dk + ["h%d" % t], ["e%d" % t], 128, [db_])
+                dma("td%d4" % t, "y", T.tab[4:128:16, :], ht[t][0:128:2], ["h%d" % t], ["tab4"], 768 * CS, 64)
+                for e in range(2):
+                    dma("td%d%d" % (t, 2 + e), "y", T.tae[2 + e:128:16, :], et[t][e:128:2], ["e%d" % t], ["tab%d" % (2 + e)], 768 * CS, 64)
+                tt("E2%d" % t, T.sw[:], pd[:, d0 + 128:d0 + 256], chv, A.mult, dk + ["h%d" % t], ["sw"], 128, [db_])
+        n = G // HA[t]
+        for h in range(HA[t]):
             for r in cl:
-                lo, hi = G * r + n * h, G * r + n * (h + 1)
-                bs = [2 * r + h] if last else [2 * r, 2 * r + 1]
                 nm = "%d%d%d" % (t, r, h)
-                gk = ["ga%d" % b for b in bs]; ck = ["cc%d" % b for b in bs]; pk = ["px%d" % b for b in bs]; xb = ["X%d" % b for b in bs]
-                if psum("a", t, r):
-                    tt("ga" + nm, T.ga[:, lo:hi], T.xa4[:, lo:hi], T.px[:, lo:hi], A.subtract, ["xa%d" % r] + pk, gk, n, xb)
+                lo, hi = 3 * n * h, 3 * n * (h + 1)
+                gav = T.ga[:, G * r + n * h:G * r + n * (h + 1)]
+                gk = ["ga%d%d" % (r, k) for k in range(2) if HA[t] == 1 or k == h]
+                x, xk = own(t, r, n * h, n * (h + 1))
+                if GT and r == t:
+                    bs = [2 + k for k in range(2) if HA[t] == 1 or k == h]
+                    tt("ga" + nm, gav, T.xa4[:, n * h:n * (h + 1)], T.px[:, G + n * h:G + n * (h + 1)], A.subtract,
+                       ["xa4"] + ["px%d" % b for b in bs], gk, n, ["X%d" % b for b in bs])
                 else:
-                    x, xk = own(t, r, n * h, n * (h + 1))
-                    tt("ga" + nm, T.ga[:, lo:hi], win.indirect(oa(r, n // 16 * h, n // 16 * (h + 1))), x, A.subtract,
-                       wk + xk + ["of%d%d" % (t, r)], gk, n, kind="h")
-                ts("cl" + nm, T.cc[:, lo:hi], T.ga[:, lo:hi], 2.0, 7.0, A.max, A.min, gk, ck, n // 2)
-                va = "%d%d" % (t, r) in CFG["va"]
-                if not va:
-                    for b in bs:
-                        base("pr%d%d" % (t, b), t, b, r == t + 1, False)
-                mm("ac" + nm, [(T.px[:, 512 * b:512 * (b + 1)], I1, T.cc[:, 512 * b:512 * (b + 1)], 512, True) for b in bs],
-                   ck + pk + ["di0"], pk, xb, opens=va)
+                    tt("ga" + nm, gav, win.indirect(lst(r, 0, n // 16 * h, n // 16 * (h + 1))), x, A.subtract, wk + xk + ["ov%d%d" % (t, r)], gk, GA * n)
+                ts("cl" + nm, cc[t][:, lo + r:hi:3], gav, 2.0, 7.0, A.max, A.min, gk, ["cc" + nm], n // 2)
+        if not last and XT[t]:
+            r = t + 1
+            for h in range(2):
+                grow(t, "%dt%d" % (t, h), XT[t][h], slice(1536 * h + r, 1536 * (h + 1), 3), T.xt[:, 512 * h:512 * (h + 1)],
+                     ["cc%d%d%d" % (t, r, h * HA[t] // 2)], ["xt%d" % h], 2 + h if GT else None)
+        if last:
+            for k in range(AD[-1]):
+                c = slice(512 * k, 512 * (k + 1))
+                dma("st_x%d" % k, "y", T.yx[:, c], w[t][:, c], wtok(t, c.start, c.stop), ["yx%d" % k], 128 * 2048)
+            for h, (lo, hi) in enumerate(zip(AD, AD[1:])):
+                c = slice(512 * lo, 512 * hi)
+                op("ad%d" % h, "G", lambda q, c=c: q.dma_start(T.yx[:, c], cc[t][:, c], accum_op=A.add),
+                   ["yx%d" % k for k in range(lo, hi)] + cck(t, range(lo, hi)), [], cost=(128 * 2048 * (hi - lo) * ACC, 128))
+        if True:
+            for k in range(AD[-1] if last else 0, 6):
+                nm = "%d%d" % (t, k)
+                c = slice(512 * k, 512 * (k + 1))
+                out = (T.yxs if last else w[t + 1])[:, c]
+                tok = ["w%d_%d" % (t + 1, k)]
+                grow(t, nm, ADD[t][k], c, out, cck(t, [k]), tok)
                 if last:
-                    act("xc" + nm, T.yxs[:, 1536 * h + r:1536 * (h + 1):3], T.px[:, lo:hi], F.Identity, -2.0 * ST, 1.0, pk, ["yx%d%d" % (h, r)], n, xb)
-                else:
-                    k = "%d%d" % (t + 1, r)
-                    lag = -LAG if r == t + 1 else 0.0
-                    if va:
-                        tt("xc" + nm, w[t + 1][:, lo:hi], T.px[:, lo:hi], wt[:, lo:hi], A.add, pk + wk[:-1], ["w" + k], n, xb)
-                    else:
-                        act("xc" + nm, w[t + 1][:, lo:hi], T.px[:, lo:hi], F.Identity, lag, 1.0, pk, ["w" + k], n, xb)
-                    if psum("a", t + 1, r) and psum("b", t + 1, r):
-                        pass
-                    elif k in CFG["xs"] and not va:
-                        act("xd" + k, xs[t + 1][:, lo:hi], T.px[:, lo:hi], F.Identity, lag, 1.0, pk, ["xs" + k], n, xb)
-                    else:
-                        dma("xd" + k, "y", xs[t + 1][:, lo:hi], w[t + 1][:, lo:hi], ["w" + k], ["xs" + k], 128 * G * 4, 128)
-            if last:
-                dma("st_x%d" % h, "y", T.yx[:, 1536 * h:1536 * (h + 1)], T.yxs[:, 1536 * h:1536 * (h + 1)], ["yx%d%d" % (h, r) for r in range(3)], [], 128 * 1536 * 4, 128)
+                    dma("st_x%d" % k, "y", T.yx[:, c], out, tok, [], 128 * 2048)
         if not last:
             ghosts(t + 1)
+            for k in range(6):
+                c = slice(512 * k, 512 * (k + 1))
+                dma("xd%d%d" % (t + 1, k), "y", xs[t + 1][:, c], w[t + 1][:, c], ["w%d_%d" % (t + 1, k)] + ["iss%d" % (t + 1)] * (k >= XH[t]),
+                    ["xs%d_%d" % (t + 1, k)], 128 * 2048)
         for r in [(t + 1 + j) % 3 for j in range(3)]:
             nm = "%d%d" % (t, r)
-            for j in range(2):
-                gather("R%s%d" % (nm, j), "sv", T.rg[:, G * (2 * r + j):G * (2 * r + j + 1)], T.tab[:, 0:W], off[t][:, 256 * r + 128 + 64 * j:256 * r + 192 + 64 * j],
-                       ["tab0", "tab1", "tab2", "of" + nm], ["R%d%d" % (r, j)], G)
-            s = slot[0]; slot[0] = 1 - s
-            b0 = 256 * s
-            pA, pB, pC, pD = [T.pb[:, b0 + 64 * k:b0 + 64 * (k + 1)] for k in range(4)]
-            gr = T.gg[:, 64 * r:64 * (r + 1)]
-            sv = T.sg[:, 64 * r:64 * (r + 1)]
-            d = [dg[t][:, k, 64 * r:64 * (r + 1)] for k in range(4)]
-            chv = T.ch[:, t, 64 * r:64 * (r + 1)]
-            mm("A" + nm, fold(pA, 2, T.rg, G * 2 * r), ["R%d0" % r, "win2"], ["pA%d" % s], ["PB"])
-            mm("B" + nm, fold(pB, 2, T.rg, G * (2 * r + 1)) + [(pB, I1, gr, 64, False)], ["R%d1" % r, "win2", "G%d" % r, "di0"], ["pB%d" % s], ["PB"])
-            act("S" + nm, sv, pB, F.Sign, -8191.5, 1.0, ["pB%d" % s], ["sg%d" % r], 64, ["PB"])
-            tc = [(pC, I16K, sv, 64, True), (pC, I1, d[1], 64, False), (pC, I16, d[3], 64, False), (pC, IM16, gr, 64, False)]
-            rd = ["sg%d" % r, "G%d" % r, "dg" + nm, "di0", "di1", "di3", "di4"]
-            if r == t:
-                tc += [(pC, I16K, chv, 64, False), (pC, I16K, chv, 64, False),
-                       (pD, I1, d[0], 64, True), (pD, I16, d[2], 64, False), (pD, IM16, gr, 64, False), (pD, I16K, chv, 64, False)]
-                rd += ["ch%d" % t]
-            mm("C" + nm, tc, rd, ["pC%d" % s], ["PB"])
-            k2 = 128 if r == t else 64
-            nv = T.nn[:, 128 * r:128 * (r + 1)]
-            tt("m1" + nm, nv, T.pb[:, b0:b0 + 128], pf[t][:, 128 * r:128 * (r + 1)], A.max, ["pA%d" % s, "pB%d" % s, "pf" + nm], ["nn%d" % r], 128, ["PB"])
-            tt("m2" + nm, T.nn[:, 128 * r:128 * r + k2], T.pb[:, b0 + 128:b0 + 128 + k2], T.nn[:, 128 * r:128 * r + k2], A.max, ["pC%d" % s, "nn%d" % r], ["nn%d" % r], k2, ["PB"])
-            if not last:
-                digits(t + 1, r, T.nn, "nn%d" % r)
+            turn = r == t
+            for j in (1, 0):
+                o = T.rg[:, G * (2 * r + j):G * (2 * r + j + 1)]
+                src = (T.tae, T.tab)[j][:, 0:48 * CS].indirect(lst(r, 2 + j))
+                tk = (["tab2", "tab3"], ["tab0", "tab1", "tab4"])[j]
+                if "%d%d" % (r, j) in RV[t].split():
+                    cp("R%s%d" % (nm, j), o, src, tk + ["ou" + nm], ["R%d%d" % (r, j)], GA * G)
+                else:
+                    act("R%s%d" % (nm, j), o, src, F.Copy, 0.0, 1.0, tk + ["ou" + nm], ["R%d%d" % (r, j)], GA * G)
+            chs = seg(ht[t], r)
+            hk = ["h%d" % t] if turn else []
+            gr, s1, s2 = T.gt[:, r, :], T.sg[:, r, 0:128], T.sg[:, r, 128:256]
+            pa, pb = T.pp[:, 0:128], T.py[:, 128 * r:128 * (r + 1)]
+            xa, xb = T.xm[:, r, 0:128], T.xm[:, r, 128:256]
+            mm("B" + nm, fold(T.py, 128 * r, 2, T.rg, G * (2 * r + 1), [(IF, half(T.gt, r))] + [(IM2F, chs)] * (2 * turn)),
+               ["R%d1" % r, "G%d" % r, "di2", "di8"] + hk + wk_[2], ["Q%d" % r], ["PY"])
+            act("S" + nm, s1, pb, F.Sign, 0.5 - LOW, 1.0, ["Q%d" % r], ["sa%d" % r], 128, ["PY"])
+            act("U" + nm, s2, pb, F.Sign, -2.5 * FL - LOW, 1.0, ["Q%d" % r], ["sb%d" % r], 128, ["PY"])
+            tt("mb" + nm, xb, pb, T.db[:, r, :], A.max, ["Q%d" % r, "db%d" % r], ["xmb%d" % r], 128, ["PY"])
+            relu = str(r) in MA[t]
+            mm("A" + nm, [(pa, IF, T.ones[:, 0:128], 128, True), (pa, IF, gr, 128, False)] + [(pa, IM1, T.db[:, r, :], 128, False)] * relu
+               + fold(T.pp, 0, 1, T.rg, G * 2 * r, [(I1, seg(T.da, r))] + [(IM2F, chs)] * turn, own=False),
+               ["R%d0" % r, "da%d" % r, "db%d" % r, "G%d" % r, "ones", "di0", "di1", "di2", "di8"] + hk + wk_[1], ["P"], ["PP"], closes=False)
+            mm("C" + nm, [(pa, IMF, s1, 128, False)], ["sa%d" % r, "P", "di3"], ["P"], ["PP"])
+            if relu:
+                act("ma" + nm, xa, pa, F.Relu, 0.0, 1.0, ["P"], ["xma%d" % r], 128, ["PP"])
             else:
-                c = slice(128 * r, 128 * (r + 1))
-                ts("f_p%d" % r, T.lh[:, r, 0:128], nv, 4095, None, A.bitwise_and, None, ["nn%d" % r], ["lo%d" % r], 128)
-                ts("f_r%d" % r, T.lh[:, r, 128:256], nv, 10, 3, A.arith_shift_right, A.bitwise_and, ["nn%d" % r], ["hi%d" % r], 128)
-                ts("f_y%d" % r, T.ua[:, c], T.lh[:, r, 0:128], 3071.0, 2.0, A.min, A.mult, ["lo%d" % r, "ua"], ["fa%d" % r], 128)
-                ts("f_t%d" % r, T.ub[:, c], T.lh[:, r, 128:256], 2.0, -3071.0, A.min, A.mult, ["hi%d" % r, "ub"], ["fb%d" % r], 128)
-                tt("f_s%d" % r, T.ua[:, c], T.ua[:, c], T.lh[:, r, 0:128], A.add, ["fa%d" % r, "lo%d" % r], ["fa%d" % r], 256)
-                for u in range(2):
-                    cu = slice(128 * r + u, 128 * (r + 1), 2)
-                    tt("f_v%d%d" % (r, u), T.s1[:, 128 * r + 64 * u:128 * r + 64 * (u + 1)], T.ub[:, cu], T.ua[:, cu], A.add,
-                       ["fa%d" % r, "fb%d" % r, "s2a"], ["fv%d%d" % (r, u)], 128)
-                op("f_x%d" % r, "v", lambda q, e, c=c: q.transpose(T.uc[:, c], T.s1[:, c]), ["fv%d0" % r, "fv%d1" % r, "uc"], ["fc%d" % r], cost=("e", 128))
-                for u in range(2):
-                    cp("f_o%d%d" % (r, u), T.rawo[:, :, 48 * u + r:48 * (u + 1):3], T.uc[:, 128 * r + 64 * u:128 * r + 64 * (u + 1)], ["fc%d" % r], ["ro%d%d" % (r, u)], 64)
+                tt("ma" + nm, xa, pa, T.db[:, r, :], A.max, ["P", "db%d" % r], ["xma%d" % r], 128, ["PP"])
+            if last:
+                for j in (1, 0):
+                    d = j + 2 * (r % 2)
+                    pv, pk, bk = T.px[:, 512 * d:512 * d + 64], ["px%d" % d], "X%d" % d
+
+                    def part(l, x):
+                        return [((T.px[:, 512 * d + 32 * u:512 * d + 32 * (u + 1)]), l(b), x(b, u), 64, False) for u in range(2) for b in range(2)]
+
+                    def cols(buf, c0): return lambda b, u: buf[:, r, c0 + 64 * b + u:c0 + 64 * (b + 1):2]
+                    up, dn, one = (lambda b: T.wf[:, 0, b, :]), (lambda b: T.wf[:, 1, b, :]), (lambda b: T.wm[:, b, :])
+                    terms = [(pv, (IKA, IKB)[j], T.k49[:], 64, True)]
+                    if j:
+                        terms += part(dn, cols(T.sg, 0)) + 2 * part(dn, cols(T.sg, 128))
+                        terms += part(one, lambda b, u: T.sw[:, 64 * b + u:64 * (b + 1):2]) * turn
+                    else:
+                        terms += part(up, cols(T.sg, 0)) + part(dn, cols(T.gt, 0)) + 2 * turn * part(up, lambda b, u: ht[t][:, b, r, u:64:2])
+                        terms += part(one, cols(T.db, 0)) * relu
+                    mm("fu%d%d" % (r, j), terms, ["db%d" % r, "k49", "di11", "di12", "wf0", "wf1", "wm0", "wm1", "sa%d" % r] + (["sb%d" % r] + ["sw"] * turn if j else ["G%d" % r] + hk),
+                       pk, [bk], closes=False)
+                    mm("fv%d%d" % (r, j), part(one, cols(T.xm, 128 * j)), ["xm%s%d" % ("ab"[j], r)] + pk, pk, [bk])
+                    for u in range(2):
+                        op("fx%d%d%d" % (r, j, u), "v", lambda q, r=r, j=j, u=u, d=d: q.transpose(
+                            T.rawo[:, 2 * j:2 * j + 2, 48 * u + r:48 * (u + 1):3], T.px[:, 512 * d + 32 * u:512 * d + 32 * (u + 1)]), pk, ["ro%d%d%d" % (r, j, u)], [bk])
+                continue
+            fa, fb = T.pf[:, 0:128], T.pf[:, 128:256]
+            mm("M" + nm, [(fb, I1, xb, 128, True), (fb, IMH, s1, 128, False), (fb, IMF, s2, 128, False)] + [(fb, I1, T.sw[:], 128, False)] * turn,
+               ["xmb%d" % r, "sa%d" % r, "sb%d" % r, "di0", "di3", "di7"] + ["sw"] * turn, ["M"], ["PF"])
+            terms = [(fa, IH, s1, 128, True), (fa, IMH, gr, 128, False)] + [(fa, I1, T.db[:, r, :], 128, False)] * relu
+            terms += [(T.pf[:, 64 * b:64 * (b + 1)], IF, chs(b), 64, False) for b in range(2 * turn)] + [(fa, I1, xa, 128, False)]
+            mm("N" + nm, terms, ["xma%d" % r, "sa%d" % r, "G%d" % r, "di0", "di2", "di4", "di7"] + hk + ["db%d" % r] * relu, ["N"], ["PF"])
+            act("db%d%d" % (t + 1, r), T.db[:, r, :], fb, F.Identity, -1.5 * FL, 1.0, ["M"], ["db%d" % r], 128, ["PF"])
+            act("da%d%d" % (t + 1, r), T.da[:, :, r, 0:64], fa, F.Identity, -FL, 1.0, ["N"], ["da%d" % r], 128, ["PF"])
+            offsets(t + 1, r)
     for k in range(4):
-        dma("st_p%d" % k, "ya", (T.ya, T.yb)[k // 2][k % 2::2, :], T.rawo[:, k, :], ["ro%d%d" % (r, u) for r in range(3) for u in range(2)], [], 128 * 384, 128)
+        dma("st_p%d" % k, "ya"[k % 2], (T.ya, T.yb)[k // 2][k % 2::2, :], T.rawo[:, k, :], ["ro%d%d%d" % (r, k // 2, u) for r in range(3) for u in range(2)], [], 128 * 384)
     return ops
 
 
-QUEUE = {"v": "v", "s": "s", "a": "s", "t": "t", "y": "y", "g": "g", "r": "g"}
+QUEUE = {"v": "v", "s": "s", "a": "s", "t": "t", "y": "y", "g": "g", "G": "g", "r": "g", "i": "g", "n": "n"}
 
 
-def depend(seq):
+def depend(seq, banks):
     wrote, read, bank, deps = {}, {}, {}, []
-    for k, (o, e) in enumerate(seq):
+    for k, o in enumerate(seq):
         d = set()
         for x in o["rd"]:
             if x in wrote: d.add(wrote[x])
         for x in o["wr"]:
             if x in wrote: d.add(wrote[x])
             d.update(read.get(x, []))
-        for b in o["banks"]:
-            d.update(j for q, j in bank.setdefault(b, {}).items() if q != e)
-            bank[b][e] = k
+        if banks:
+            for b in o["banks"]:
+                d.update(j for q, j in bank.setdefault(b, {}).items() if q != o["eng"])
+                bank[b][o["eng"]] = k
         for x in o["rd"]:
             read.setdefault(x, []).append(k)
         for x in o["wr"]:
@@ -377,38 +473,207 @@ def depend(seq):
     return deps
 
 
+def times(o):
+    e, c = o["eng"], o["cost"]
+    if e in "ni":
+        return 0.0, 0.0, 0.0
+    if e in "yaGr":
+        return {"y": 60.0, "a": 60.0, "G": 900.0, "r": 400.0}[e], (c[0] / 25.0 + 25.0 * c[1]) / 16, 1200.0
+    return (0.0 if e == "t" else 30.0) + 0.83 * max(c, 64), 0.0, 80.0
+
+
+def names(q):
+    out = []
+    for t, line in enumerate(q):
+        for x in line.split():
+            s = t - x.startswith("-")
+            x = x.lstrip("-")
+            for c, r in (("T", s), ("N", s + 1), ("O", s + 2)):
+                x = x.replace("." + c, "%d%d" % (s, r % 3)).replace(":" + c, "%d%d" % (s + 1, r % 3))
+            out.append(x.replace("#", str(s)).replace("+", str(s + 1)))
+    return out
+
+
+def place(ops, tm, before, rank, back):
+    used, start = {}, {}
+    for k in rank:
+        o = ops[k]
+        hold, move, lat = tm[k]
+        whole = hold + move + lat
+        need = [(QUEUE[o["eng"]], 0.0, hold, None)] + [(b, 0.0, whole, o["eng"]) for b in o["banks"]] + ([("d", hold + lat / 2, move, None)] if move else [])
+        if back:
+            need = [(r, whole - a - n, n, e) for r, a, n, e in need]
+        t = max([0.0] + [start[j] + gap for j, gap in before[k].items()])
+        moved = True
+        while moved:
+            moved = False
+            for r, a, n, e in need:
+                for lo, hi, who in used.get(r, []):
+                    if lo < t + a + n - 1e-6 and t + a < hi - 1e-6 and (e is None or e != who):
+                        t = hi - a; moved = True
+        for r, a, n, e in need:
+            if n:
+                used.setdefault(r, []).append((t + a, t + a + n, e))
+        start[k] = t
+    return start
+
+
+def order(ops):
+    n = len(ops)
+    tm = [times(o) for o in ops]
+    deps = [{j: sum(tm[j]) for j in d} for d in depend(ops, False)]
+    after = [{} for _ in ops]
+    for k in range(n):
+        for j in deps[k]:
+            after[j][k] = sum(tm[k])
+    index = {o["name"]: k for k, o in enumerate(ops)}
+    for q in LISTS:
+        line = [index[x] for x in names(q)]
+        for j, k in zip(line, line[1:]):
+            deps[k].setdefault(j, tm[j][0])
+            after[j].setdefault(k, tm[j][0] + sum(tm[k]) - sum(tm[j]))
+    way = [0.0] * n
+    left, todo = [len(x) for x in after], [k for k in range(n) if not after[k]]
+    for k in todo:
+        way[k] = 1.0 + max([sum(tm[k])] + [way[j] + deps[j][k] for j in after[k]])
+        for j in deps[k]:
+            left[j] -= 1
+            if not left[j]:
+                todo.append(j)
+    assert len(todo) == n, [ops[k]["name"] for k in range(n) if left[k]][-12:]
+    rank = sorted(range(n), key=lambda k: -way[k])
+    best = None
+    for _ in range(TURNS):
+        start = place(ops, tm, deps, rank, False)
+        end = max(start[k] + sum(tm[k]) for k in range(n))
+        if best is None or end < best[0]:
+            best = (end, start, max(way))
+        late = place(ops, tm, after, sorted(range(n), key=lambda k: (-start[k], way[k])), True)
+        rank = sorted(range(n), key=lambda k: (-late[k] - sum(tm[k]), -way[k]))
+    EST.append(best)
+    return [ops[k] for k in sorted(range(n), key=lambda k: (best[1][k], -way[k]))]
+
+
+def improve(ops, seq):
+    n = len(ops)
+    tm = [times(o) for o in ops]
+    deps = depend(ops, False)
+    anc = [0] * n
+    for k in range(n):
+        for j in deps[k]:
+            anc[k] |= anc[j] | (1 << j)
+    qn = ["vstygn".index(QUEUE[o["eng"]]) for o in ops]
+    bn = {b: i for i, b in enumerate(sorted(set(b for o in ops for b in o["banks"])))}
+    bk = [[3 * bn[b] for b in o["banks"]] for o in ops]
+    other = [[b + e for b in bk[k] for e in range(3) if e != qn[k]] for k in range(n)]
+
+    def run(seq):
+        free, who, bank, fin, why = [0.0] * 7, [n] * 7, [n] * (3 * len(bn)), [0.0] * (n + 1), [0] * n
+        for k in seq:
+            hold, move, lat = tm[k]
+            q = qn[k]
+            t, y = free[q], who[q]
+            for b in other[k]:
+                if fin[bank[b]] > t:
+                    y = bank[b]; t = fin[y]
+            for j in deps[k]:
+                if fin[j] > t:
+                    t, y = fin[j], j
+            t += hold
+            free[q], who[q] = t, k
+            if move:
+                t += lat / 2
+                if free[6] > t:
+                    t, y = free[6], who[6]
+                free[6], who[6] = t + move, k
+                fin[k] = t + move + lat / 2
+            else:
+                fin[k] = t + lat
+            why[k] = y
+            for b in bk[k]:
+                bank[b + q] = k
+        return fin, why
+
+    x = SEED
+    fin, why = run(seq)
+    now = max(fin)
+    best = (now, seq)
+    for it in range(SWAPS):
+        k, pairs = fin.index(now), []
+        while k != n:
+            j = why[k]
+            if j != n and not anc[k] >> j & 1:
+                pairs.append((j, k))
+            k = j
+        x = (x * 6364136223846793005 + 1442695040888963407) % 2 ** 64
+        u, v = pairs[(x >> 40) % len(pairs)]
+        pu, pv = seq.index(u), seq.index(v)
+        part = seq[pu:pv + 1]
+        if x >> 33 & 1:
+            go = [k == v or anc[v] >> k & 1 for k in part]
+        else:
+            go = [not (k == u or anc[k] >> u & 1) for k in part]
+        new = seq[:pu] + [k for k, y in zip(part, go) if y] + [k for k, y in zip(part, go) if not y] + seq[pv + 1:]
+        f, y = run(new)
+        end = max(f)
+        if end <= now + (HEAT * (1 - it / SWAPS) ** 2 + 5.0) * -math.log(((x >> 8) % 2 ** 20 + 1) / 2 ** 20):
+            seq, fin, why, now = new, f, y, end
+            if end < best[0]:
+                best = (end, new)
+    EST.append((best[0], [f - sum(t) for f, t in zip(run(best[1])[0], tm)], 0))
+    return best[1]
+
+
+FOUND = {}
+ORDER = """
+ld_x0 ld_snd ld_x1 ld_x2 ld_x3 ones tae0 win0 dv0 sd0 pi t8a di0 tc pj0 wm0 wm100 pj1 dv1 di5 dq11 dv2 col1 sd1 di2 k49 zh0 snd16 ze0 col0 cv1 cv0 gg00 di10 t8c sdc ld_p3 ld_p1 wm110 wm000 t8b ld_p0 ld_p2 dq10 dq01 tab0 gg01 sh01 sh21 sh20 sh10 sh11 sh00 tr1 tr2 tr0 wm111 sd00 sd01 dq00 vs1 vs0 cq di1 di6 win01 i321 win10 i320 arr0 cv3 ov02 cv2 ov01 ov00 win20 win21 cp00 wm101 wm010 ze1 wm011 wm001 zh1 zh2 ze2 win00 di11 xa00 dg02 dg01 dg00 da02 db00 po1 db02 dag win11 da00 vp00 c20 pu00 ga001 ou00 ga020 da01 G00 db01 gm di12 wf1 wf0 di7 D0 v20 pu01 po0 ch0 ga010 E10 ou01 pu02 cl001 cl020 ou02 ga000 cp01 cl000 cl010 ga011 ga021 cl011 cl021 td01 td00 td04 di4 di3 di9 di8 R011 R021 pr0t1 pr0t0 td02 td03 vp01 G01 ac01 B01 ac00 R010 E20 mb01 A01 xc00 xc01 gg11 S01 C01 ma01 cp02 U01 gg10 ac0t0 M01 N01 ac03 da11 db11 R020 xc0t0 xc03 ac0t1 pu11 xc0t1 ac02 pv11 xc02 ac05 ac04 vp02 ov11 xc05 xc04 sd11 sd10 arr1 G02 iss1 D1 B02 xa11 S02 U02 R001 xd13 xd15 xd12 xd10 xd14 xd11 ou11 cp11 A02 C02 vp11 ga110 mb02 cl110 ma02 M02 N02 db12 da12 G11 R000 B00 pv12 c21 ga111 ov12 cl111 v21 pu12 mb00 ch1 ou12 E11 ga120 A00 S00 U00 C00 ma00 M00 N00 da10 db10 pr1t0 pv10 pr1t1 td12 td13 td14 td10 td11 R120 cl120 cp12 E21 ga121 ov10 cl121 ga100 ga101 cl100 pu10 ac1t0 ac1t1 vp12 R121 xc1t1 G12 ac11 xc1t0 cl101 B12 xc11 ou10 gg20 mb12 cp10 S12 U12 gg21 A12 ac13 C12 M12 ac10 ma12 vp10 xc13 ac15 N12 R101 xc10 ac12 G10 db22 da22 R100 xc15 B10 pu22 xc12 ac14 mb10 ou22 pv22 sd20 sd21 iss2 arr2 xc14 ov22 cp22 U10 S10 xa22 A10 M10 D2 C10 ma10 N10 vp22 c22 xd22 xd23 xd20 xd21 xd24 xd25 st_x0 R111 G22 da20 db20 R110 v22 pu20 pv20 B11 A11 ga220 ga221 ch2 ov20 E12 cl220 ou20 cl221 mb11 ga200 S11 U11 C11 ma11 M11 N11 da21 db21 pu21 pv21 cp20 ov21 cl200 ga210 ou21 cl210 vp20 td24 td22 td23 st_x1 td21 td20 st_x2 st_x4 st_x5 st_x3 R200 G20 R201 cp21 R211 R221 A20 B20 vp21 S20 U20 G21 C20 fu01 mb20 ma20 ga201 ga211 cl201 cl211 B22 B21 R210 U21 S21 fv01 A21 E22 fu10 C21 fu00 fu11 ma21 fx010 mb21 mb22 R220 S22 U22 ad0 A22 fv00 fx011 fu21 fv11 C22 fv21 fx000 fx001 fx111 fx110 fx211 fx210 ad1 ad2 fu20 fv10 ma22 fx101 fx100 fv20 fx201 fx200 st_p3 st_p2 st_p0 st_p1
+"""
+
+
 def rank_program(g, core, T, topo):
     if T.rank_of(core) is None:
         return
-    ops = build(g, T, topo, core)
-    byname = {o["name"]: o for o in ops}
-    seq = [(byname[x[:-2]], x[-1]) for x in ORDER.split()]
-    assert len(seq) == len(ops) == len(byname)
-    deps = depend(seq)
+    ops = build(T, topo, core)
+    if not FOUND:
+        index = {o["name"]: k for k, o in enumerate(ops)}
+        FOUND[0] = [index[x] for x in ORDER.split()]
+        assert sorted(FOUND[0]) == list(range(len(ops)))
+    seq = [ops[k] for k in FOUND[0]]
+    deps = depend(seq, True)
     qs = {"v": g.vector, "s": g.scalar, "t": g.tensor, "y": g.sync, "g": g}
-    needed = set(j for k, d in enumerate(deps) if seq[k][1] != "n" for j in d)
+    needed = set(j for k, d in enumerate(deps) if seq[k]["eng"] != "n" for j in d)
     done, count, waited, sent = {}, {"v": 0, "s": 0, "t": 0, "g": 0}, {}, 0
-    for k, (o, e) in enumerate(seq):
+    for k, o in enumerate(seq):
+        e = o["eng"]
         if e == "n":
-            done[k] = (o["name"], o["cost"][1])
+            done[k] = (o["name"], o["cost"])
+            continue
+        if e == "i":
+            if k in needed:
+                g.sem_inc(T.sem[o["name"]], 1); done[k] = (o["name"], 1)
             continue
         qn = QUEUE[e]
         need = {}
         for j in deps[k]:
+            if seq[j]["eng"] == "r" or (e == "t" and seq[j]["eng"] == "t" and not set(seq[j]["wr"]) - set(o["rd"])):
+                continue
             s, v = done[j]
             need[s] = max(need.get(s, 0), v)
         for s, v in need.items():
             if waited.get((qn, s), 0) < v:
                 qs[qn].wait_ge(T.sem[s], v); waited[(qn, s)] = v
-        ins = o["fn"](qs[qn], e)
+        ins = o["fn"](qs[qn])
         if e == "r":
             sent += len(topo.engines(core, T.cores[(T.rank_of(core) - 1) % len(T.cores)]))
-        elif e in "ya":
+        elif e in "yaG":
             ins.then_inc(T.sem[o["name"]], 16); done[k] = (o["name"], 16)
         elif k in needed:
             count[e] += 1
             ins.then_inc(T.sem["q" + e], 1); done[k] = ("q" + e, count[e])
     g.wait_ge(T.sem.sent, sent)
-    for k, (o, e) in enumerate(seq):
-        if e in "ya" and k not in needed:
+    for k, o in enumerate(seq):
+        if o["eng"] in "yaG" and k not in needed:
             g.wait_ge(T.sem[o["name"]], 16)
+    for e, v in count.items():
+        if max([x for (q, s), x in waited.items() if s == "q" + e] + [0]) < v:
+            g.wait_ge(T.sem["q" + e], v)

import math
from concourse.bass import DstId, RemoteDMATransfer
from concourse.mybir import AluOpType as A, ActivationFunctionType as F

V, G, W, ST = 3072, 1024, 4096, 3
CS = 88
FL, LOW = 88.0, -96.0
XCH = 4
GH = 2
HA = (2, 2, 2)
ADD = ("vvvvvv", "vvvvvv", "d")
GT = True
SB = ("", "", "")
GS = "ss"
XT = ("ss", "ss")
RV = ("", "", "21")
TURNS, SWAPS, HEAT, SEED = 3, 200000, 150.0, 7
FOLD, ACC = 0.3, 1.5
AD = (0, 3, 5, 6)
XH = (1, 1)
G0 = (0, 256, 1024)
MA = ("", "", "")
EST = []
LISTS = [["cp.T c2# ga.T0 ch# E1# ga.N0 ga.O0 cp.N ga.N1 ga.T1 ga.O1 cp.O",
          "cp.T c2# ga.T0 ch# E1# ga.T1 ga.N0 ga.N1 cp.N ga.O0 ga.O1 cp.O",
          "cp.T c2# ga.T0 ch# E1# ga.T1 cp.N ga.N0 ga.O0 ga.N1 ga.O1 cp.O"],
         ["xa.T R.N1 R.N0 R.O1 R.O0", "xa.T -R.T1 -R.T0 R.N0 R.N1 R.O1 R.O0", "xa.T -R.T1 -R.T0 R.N0 R.N1 R.O1 R.O0 R.T0"]]

SCRATCH = {
    "xraw": ("sbuf", [128, V], "int32"), "sndr": ("sbuf", [128, 64], "int32"),
    "raw": ("sbuf", [128, 4, 96], "int32"), "rawo": ("sbuf", [128, 4, 96], "float32"),
    "w0": ("sbuf", [128, W], "float32"), "w1": ("sbuf", [128, W], "float32"), "w2": ("sbuf", [128, W], "float32"),
    "xs1": ("sbuf", [128, V], "float32"), "xs2": ("sbuf", [128, V], "float32"), "yxs": ("sbuf", [128, V], "float32"),
    "gs0": ("sbuf", [128, G], "float32"), "gs1": ("sbuf", [128, G], "float32"), "gs2": ("sbuf", [128, G], "float32"),
    "gsm": ("sbuf", [128, G], "float32"), "xa4": ("sbuf", [128, G], "float32"), "xb": ("sbuf", [128, G], "float32"), "xt": ("sbuf", [128, G], "float32"),
    "ga": ("sbuf", [128, V], "bfloat16"), "cp": ("sbuf", [128, V], "bfloat16"), "c2": ("sbuf", [128, G], "bfloat16"),
    "cc0": ("sbuf", [128, V], "bfloat16"), "cc1": ("sbuf", [128, V], "bfloat16"), "cc2": ("sbuf", [128, V], "bfloat16"),
    "tab": ("sbuf", [128, 48 * CS], "bfloat16"), "tae": ("sbuf", [128, 48 * CS], "bfloat16"), "rg": ("sbuf", [128, 2 * V], "bfloat16"),
    "ones": ("sbuf", [128, 512], "bfloat16"),
    "k49": ("sbuf", [128, 64], "bfloat16"), "wf": ("sbuf", [128, 2, 2, 128], "bfloat16"),
    "di": ("sbuf", [128, 13, 128], "bfloat16"), "i32": ("sbuf", [128, 2, 128], "float32"),
    "win": ("sbuf", [128, 3, 144], "bfloat16"), "wm": ("sbuf", [128, 4, 128], "bfloat16"),
    "dq": ("sbuf", [128, 2, 128], "bfloat16"), "dv": ("sbuf", [128, 2, 128], "float32"),
    "t8a": ("sbuf", [128, 8], "bfloat16"), "t8b": ("sbuf", [128, 8], "bfloat16"), "t8c": ("sbuf", [128, 8], "bfloat16"),
    "pi": ("sbuf", [128, 1], "int32"), "pj": ("sbuf", [128, 2], "int32"), "col": ("sbuf", [128, 2], "float32"),
    "sd": ("sbuf", [128, 2, 3, CS], "bfloat16"), "tc": ("sbuf", [128, 2, 3, CS], "bfloat16"),
    "da": ("sbuf", [128, 2, 3, CS], "bfloat16"), "db": ("sbuf", [128, 3, 128], "bfloat16"),
    "e0": ("sbuf", [128, 2, 3, CS], "bfloat16"), "e1": ("sbuf", [128, 2, 3, CS], "bfloat16"), "e2": ("sbuf", [128, 2, 3, CS], "bfloat16"),
    "h0": ("sbuf", [128, 2, 3, CS], "bfloat16"), "h1": ("sbuf", [128, 2, 3, CS], "bfloat16"), "h2": ("sbuf", [128, 2, 3, CS], "bfloat16"),
    "sw": ("sbuf", [128, 128], "bfloat16"), "gt": ("sbuf", [128, 3, 128], "bfloat16"), "sg": ("sbuf", [128, 3, 256], "bfloat16"),
    "xm": ("sbuf", [128, 3, 256], "bfloat16"), "cq": ("sbuf", [128, 3, 128], "bfloat16"),
    "s1": ("sbuf", [128, 3, 128], "float32"), "s2": ("sbuf", [128, 3, 128], "float32"), "vs": ("sbuf", [128, 3, 128], "float32"),
    "offs": ("sbuf", [128, 64], "uint16"),
    "off0": ("sbuf", [128, 768], "uint16"), "off1": ("sbuf", [128, 768], "uint16"), "off2": ("sbuf", [128, 768], "uint16"),
    "px": ("psum", [128, 2048], "float32"), "pc": ("psum", [128, 512], "float32"), "py": ("psum", [128, 512], "float32"),
    "pp": ("psum", [128, 512], "float32"), "pf": ("psum", [128, 512], "float32"),
}
DMAS = (["ld_snd", "sdc"] + ["ld_x%d" % k for k in range(XCH)] + ["ld_p%d" % k for k in range(4)]
        + ["td%d%d" % (t, d) for t in range(ST) for d in range(5)] + ["st_p%d" % k for k in range(4)]
        + ["xd%d%d" % (t, k) for t in (1, 2) for k in range(6)] + ["st_x%d" % k for k in range(6)] + ["ad%d" % k for k in range(6)])
SEMAPHORES = ["qv", "qs", "qt", "qg", "sent", "arr0", "arr1", "arr2", "iss1", "iss2"] + DMAS


def build(T, topo, core):
    ops = []

    def op(name, eng, fn, rd, wr, banks=(), cost=64.0):
        ops.append({"name": name, "eng": eng, "fn": fn, "rd": list(rd), "wr": list(wr), "banks": list(banks), "cost": cost})

    dst = T.cores[(T.rank_of(core) - 1) % len(T.cores)]
    rid, pid, _ = topo.addr(dst)
    emask = topo.mask(core, dst)
    w = [T.w0, T.w1, T.w2]; gs = [T.gs0, T.gs1, T.gs2]; xs = [T.xraw, T.xs1, T.xs2]; cc = [T.cc0, T.cc1, T.cc2]
    off = [T.off0, T.off1, T.off2]; et = [T.e0, T.e1, T.e2]; ht = [T.h0, T.h1, T.h2]
    SC = (1.0, -1.0, FL, -FL, FL / 2, -48.0, -2.0 * ST, -FL / 2, -2 * FL, 4.0 - 2 * ST, 4.0, -FL - LOW, -1.5 * FL - LOW)
    I1, IM1, IF, IMF, IH, IM48, IM6, IMH, IM2F, IM2, I4, IKA, IKB = [T.di[:, k, :] for k in range(13)]
    GA = 1.56

    def dma(name, eng, out, in_, rd, wr, nbytes, rows=128):
        op(name, eng, lambda q: q.dma_start(out, in_), rd, wr, cost=(nbytes, rows))

    def ts(name, out, in0, s1, s2, o0, o1, rd, wr, n, banks=()):
        if o1 is None:
            op(name, "v", lambda q: q.tensor_scalar(out, in0, s1, None, o0), rd, wr, banks, n)
        else:
            op(name, "v", lambda q: q.tensor_scalar(out, in0, s1, s2, o0, o1), rd, wr, banks, n)

    def tt(name, out, in0, in1, o, rd, wr, n, banks=()):
        op(name, "v", lambda q: q.tensor_tensor(out, in0, in1, o), rd, wr, banks, n)

    def cp(name, out, in_, rd, wr, n, banks=()):
        op(name, "v", lambda q: q.tensor_copy(out, in_), rd, wr, banks, n)

    def act(name, out, in_, func, bias, scale, rd, wr, n, banks=()):
        op(name, "s", lambda q: q.activation(out, in_, func, bias=bias, scale=scale), rd, wr, banks, n)

    def sel(name, out, in_, pat, cmp, fill, base, cm, rd, wr, n):
        op(name, "g", lambda q: q.affine_select(out, in_, pat, cmp, fill, base, cm), rd, wr, cost=200 + 2 * n)

    def iota(name, out, pat, base, cm, rd, wr, n):
        op(name, "g", lambda q: q.iota(out, pat, base, cm, allow_small_or_imprecise_dtypes=True), rd, wr, cost=160 + 2 * n)

    def mm(name, terms, rd, wr, banks, opens=True, closes=True):
        def fn(q):
            r = None
            for k, (o, l, x, n, st) in enumerate(terms):
                last = k == len(terms) - 1 or terms[k + 1][4]
                r = q.matmul(o, l, x, bool(st and opens), bool(last and closes))
            return r
        op(name, "t", fn, rd, wr, banks, sum(x[3] + 16 for x in terms) / 2)

    def fold(buf, c0, k, src, base, more=(), own=True):
        terms = []
        for b in range(2):
            o = buf[:, c0 + 64 * b:c0 + 64 * (b + 1)]
            terms += [(o, T.win[:, k, 14 - 2 * m:142 - 2 * m], src[:, base + 2 * m + b:base + G:16], 64, own and m == 0) for m in range(8)]
            terms += [(o, l, x(b), 64, False) for l, x in more]
        return terms

    def half(buf, r):
        return lambda b: buf[:, r, 64 * b:64 * (b + 1)]

    def seg(buf, r):
        return lambda b: buf[:, b, r, 0:64]

    cw = V // XCH
    dma("ld_snd", "y", T.sndr[:], T.snd[:], [], ["sndr"], 32768)
    for k in range(XCH):
        dma("ld_x%d" % k, "ay"[k % 2], T.xraw[:, cw * k:cw * (k + 1)], T.x0[:, cw * k:cw * (k + 1)], [], ["xr%d" % k], 128 * cw * 4)
    for k in range(4):
        dma("ld_p%d" % k, "ay"[k % 2], T.raw[:, k, :], (T.la, T.lb)[k // 2][k % 2::2, :], [], ["raw%d" % k], 128 * 384)
    xr = ["xr%d" % k for k in range(XCH)]

    op("ones", "v", lambda q: q.memset(T.ones[:], 1.0), [], ["ones"], cost=256)
    op("tae0", "v", lambda q: q.memset(T.tae[:], 0.0), [], ["tab2", "tab3"], cost=24 * CS)
    act("tab0", T.tab[:], T.tae[:], F.Identity, 0.0, 1.0, ["tab2", "tab3"], ["tab0", "tab1", "tab4"], 48 * CS)
    op("win0", "v", lambda q: q.memset(T.win[:], 0.0), [], ["win"], cost=216)
    op("wm0", "v", lambda q: q.memset(T.wm[:], 0.0), [], ["wm%d" % k for k in range(4)], cost=256)
    op("dv0", "v", lambda q: q.memset(T.dv[:], 0.0), [], ["dv0", "dv1"], cost=256)
    sel("di0", I1, T.ones[:, 0:128], [[-1, 128]], A.is_equal, 0.0, 0, 1, ["ones"], ["di0"], 128)
    op("k49", "v", lambda q: q.memset(T.k49[:], 49.0), [], ["k49"])
    for k in range(1, 13):
        act("di%d" % k, T.di[:, k, :], I1, F.Identity, 0.0, SC[k], ["di0"], ["di%d" % k], 128)
    for k in range(2):
        act("i32%d" % k, T.i32[:, k, :], I1, F.Identity, 0.0, SC[k], ["di0"], ["i32%d" % k], 128)
    sel("t8a", T.t8a[:], T.ones[:, 0:8], [[-16, 8]], A.is_ge, 0.0, 0, 1, ["ones"], ["t8a"], 8)
    sel("t8b", T.t8b[:], T.t8a[:], [[16, 8]], A.is_ge, 0.0, 15, -1, ["t8a"], ["t8b"], 8)
    act("t8c", T.t8c[:], T.di[:, 2, 4:128:16], F.Identity, 0.0, 2.0, ["di2"], ["t8c"], 64)
    for e in range(2):
        act("win0%d" % e, T.win[:, 0, 14 + e:128:16], T.t8b[:], F.Identity, 0.0, 1.0, ["t8b", "win"], ["win0%d" % e], 64)
        act("win1%d" % e, T.win[:, 1, 14 + e:128:16], T.di[:, 0, 2 + e:128:16], F.Identity, 0.0, 1.0, ["di0", "win"], ["win1%d" % e], 64)
        tt("win2%d" % e, T.win[:, 2, 14 + e:128:16], T.di[:, 0, e:128:16], T.t8c[:], A.add, ["di0", "t8c", "win"], ["win2%d" % e], 64)
    wk_ = [["win%d%d" % (k, e) for e in range(2)] for k in range(3)]
    for k, ws in enumerate(((48.0, 1.0), (1.0, float(CS)))):
        for b in range(2):
            o = T.wm[:, 2 * k + b, b:128:2]
            for e in range(2):
                sel("wm%d%d%d" % (k, b, e), o, o, [[-2, 64]], A.not_equal, ws[e], -e, 1, ["wm%d" % (2 * k + b)], ["wm%d" % (2 * k + b)], 64)
    for k in range(2):
        act("wf%d" % k, T.wf[:, k], T.wm[:, 0:2, :], F.Identity, 0.0, (FL / 2, -FL / 2)[k], ["wm0", "wm1"], ["wf%d" % k], 256)
    for b in range(2):
        for e in range(2):
            act("dq%d%d" % (b, e), T.dq[:, b, e:128:2], T.di[:, (0, 5)[e], b:128:2], F.Identity, 0.0, 1.0, ["di0", "di5"], ["dq%d%d" % (b, e)], 64)
        act("dv%d" % (b + 1), T.dv[:, b, 1:128:2], T.di[:, 0, b:128:2], F.Identity, 0.0, 1.0, ["di0", "dv%d" % b], ["dw%d" % b], 64)
    op("pi", "g", lambda q: q.iota(T.pi[:], [[0, 1]], 0, 1), [], ["pi"], cost=170)
    ts("pj0", T.pj[:, 0:1], T.pi[:], 1, None, A.bitwise_and, None, ["pi"], ["pj0"], 64)
    ts("pj1", T.pj[:, 1:2], T.pi[:], 14, None, A.bitwise_and, None, ["pi"], ["pj1"], 64)
    ts("col0", T.col[:, 0:1], T.pj[:, 0:1], 49.0 * 129.0, LOW - 129.0, A.mult, A.add, ["pj0"], ["col0"], 64)
    ts("col1", T.col[:, 1:2], T.pj[:, 1:2], 3.0, LOW, A.mult, A.add, ["pj1"], ["col1"], 64)
    iota("tc", T.tc[:], [[0, 6], [1, CS]], int(LOW), 0, [], ["tc"], 6 * CS)
    iota("sd0", T.sd[:], [[1, 6], [0, CS]], 0, 0, [], ["sd"], 6 * CS)
    act("sd1", T.sd[:], T.sd[:], F.Identity, T.col[:, 1:2], 1.0, ["sd", "col1"], ["sd"], 6 * CS)
    dma("sdc", "y", T.sd[0:128:2], T.tc[0:128:2], ["tc", "sd"], ["sd"], 64 * 12 * CS, 64)
    act("dag", T.da[:, :, :, 64:CS], T.sd[:, :, :, 64:CS], F.Identity, 0.0, 1.0, ["sd"], ["dag"], 6 * (CS - 64))

    def cck(t, ks):
        return sorted(set("cc%d%d%d" % (t, r, k * HA[t] // 6) for r in range(3) for k in ks))

    def cover(lo, hi, t):
        n = cw if t == 0 else 512
        return range(lo // n, (hi + n - 1) // n)

    def wtok(t, lo=0, hi=V):
        return ["w%d_%d" % (t, k) for k in cover(lo, hi, t)]

    def xtok(t, lo=0, hi=V):
        return [("xr%d" % k if t == 0 else "xs%d_%d" % (t, k)) for k in cover(lo, hi, t)]

    def own(t, r, a, b):
        if t and r == t and XT[t - 1]:
            return T.xt[:, a:b], ["xt%d" % h for h in range(a // 512, (b + 511) // 512)]
        return xs[t][:, 3 * a + r:3 * b:3], xtok(t, 3 * a, 3 * b)

    def grow(t, nm, who, c, out, toks, tok, keep=None):
        b = nextbank() if keep is None else keep
        o = T.px[:, 512 * b:512 * (b + 1)]
        if who == "s":
            lag = [] if keep is None else [(o, (IM2, I4)[t], T.ones[:], 512, False)]
            mm("pr" + nm, [(o, T.i32[:, 0, :], w[t][:, c], 2048, True)] + lag, ["i320", "ones", "di9", "di10"] + wtok(t, c.start, c.stop), ["px%d" % b], ["X%d" % b], closes=False)
            mm("ac" + nm, [(o, I1, cc[t][:, c], 512, True)], toks + ["px%d" % b, "di0"], ["px%d" % b], ["X%d" % b], opens=False)
            act("xc" + nm, out, o, F.Identity, -4.0 if lag else -2.0 * ST if t == 0 else 0.0, 1.0, ["px%d" % b], tok, 512, ["X%d" % b])
        else:
            mm("ac" + nm, ([(o, IM6, T.ones[:], 512, True)] if t == 0 else []) + [(o, I1, cc[t][:, c], 512, t > 0)],
               toks + ["di0", "di6", "ones"], ["px%d" % b], ["X%d" % b])
            tt("xc" + nm, out, o, w[t][:, c], A.add, ["px%d" % b] + wtok(t, c.start, c.stop), tok, 512, ["X%d" % b])

    def ghosts(t):
        for h in range(GH):
            nm = "%d%d" % (t, h)
            c = slice(G0[h], G0[h + 1]) if t == 0 else slice(G // GH * h, G // GH * (h + 1))
            n = c.stop - c.start
            o = T.offs[:, c.start // 16:c.stop // 16]
            land = w[t][:, V + c.start:V + c.stop]
            if t == 0:
                cp("gg" + nm, gs[0][:, c], T.xraw[:, 0:V].indirect(o), xr + ["offs"], ["gs" + nm], GA * n)
                if GS != "ww" and h == GH - 1:
                    act("gm", T.gsm[:], gs[0][:], F.Identity, -2.0 * ST, 1.0, ["gs0%d" % k for k in range(GH)], ["gm%d" % k for k in range(GH)], G)
            elif GS[t - 1] == "w":
                act("gg" + nm, gs[t][:, c], w[t][:, 0:V].indirect(o), F.Copy, 0.0, 1.0, wtok(t) + ["offs"], ["gs" + nm], GA * n)
            elif GS[t - 1] == "s":
                act("gg" + nm, gs[t][:, c], cc[t - 1][:, 0:V].indirect(o), F.Copy, 0.0, 1.0, cck(t - 1, range(6)) + ["offs"], ["gs" + nm], GA * n)
                srcs = [T.gsm[:, c]] + [gs[k][:, c] for k in range(1, t + 1)]
                op("sd" + nm, "r", lambda q, land=land, srcs=srcs: q.remote_dma_fused([RemoteDMATransfer(
                    dst_ids=[DstId(rid=rid, pnc=pid)], dma_engine_mask=emask, remote_sem=T.sem["arr%d" % t], srcs=srcs,
                    dsts=[land], alu_op=1)], local_sem=T.sem.sent),
                   ["gm%d" % h] + ["gs%d%d" % (k, h) for k in range(1, t + 1)], ["wire" + nm], cost=(128 * n * 4 * (1 + FOLD * t), 128))
                continue
            else:
                prev, tok = (T.gsm, "gm%d" % h) if t == 1 else (gs[t - 1], "gs%d%d" % (t - 1, h))
                tt("gg" + nm, gs[t][:, c], cc[t - 1][:, 0:V].indirect(o), prev[:, c], A.add, cck(t - 1, range(6)) + ["offs", tok], ["gs" + nm], GA * n)
            op("sd" + nm, "r", lambda q, land=land, c=c: q.remote_dma(land, gs[t][:, c], T.sem["arr%d" % t], T.sem.sent, pid, rid, emask),
               ["gs" + nm], ["wire" + nm], cost=(128 * n * 4, 128))
        if t:
            op("iss%d" % t, "i", None, ["wire%d%d" % (t, h) for h in range(GH)], ["iss%d" % t])
        op("arr%d" % t, "n", None, ["wire%d%d" % (t, h) for h in range(GH)], ["wg%d" % t], cost=GH * len(topo.engines(core, dst)))

    cp("snd16", T.offs[:], T.sndr[:], ["sndr"], ["offs"], 64)
    ghosts(0)
    for t in range(ST):
        for nm, buf in (("e", et[t]), ("h", ht[t])):
            if t == 0:
                op("z%s0" % nm, "v", lambda q, buf=buf: q.memset(buf[:], 0.0), [], [nm + "0"], cost=3 * CS)
            else:
                iota("z%s%d" % (nm, t), buf[:], [[0, 6 * CS]], 0, 0, ["wire0%d" % (GH - 1)], ["%s%d" % (nm, t)], 6 * CS)
    for k in range(XCH):
        cp("cv%d" % k, T.w0[:, cw * k:cw * (k + 1)], T.xraw[:, cw * k:cw * (k + 1)], ["xr%d" % k], ["w0_%d" % k], cw)

    for r in range(3):
        for u in range(2):
            cp("sh%d%d" % (r, u), T.s1[:, r, 64 * u:64 * (u + 1)], T.raw[:, :, 48 * u + r:48 * (u + 1):3], ["raw%d" % k for k in range(4)], ["s1%d%d" % (r, u)], 64)
        op("tr%d" % r, "v", lambda q, r=r: q.transpose(T.s2[:, r, :], T.s1[:, r, :]), ["s1%d0" % r, "s1%d1" % r], ["s2%d" % r], cost=128)
    for u in range(2):
        act("vs%d" % u, T.vs[:, :, u:128:2], T.s2[:, :, 64 * u:64 * (u + 1)], F.Identity, 0.0, 1.0, ["s20", "s21", "s22"], ["vs%d" % u], 192)
    act("cq", T.cq[:], T.vs[:], F.Identity, 129.0 - 23.5 / 48.0, 1.0 / 48.0, ["vs0", "vs1"], ["cq"], 384)
    for r in range(3):
        cp("ov0%d" % r, off[0][:, 256 * r:256 * r + 128], T.vs[:, r, :], ["vs0", "vs1"], ["ov0%d" % r], 128)
        terms = []
        pd, pk, bk = ((T.pp, ["P"], "PP"), (T.py, ["Q0", "Q1"], "PY"), (T.pc, ["cnt0", "cnt1"], "PC"))[r]
        for j in range(2):
            for b in range(2):
                o = pd[:, 128 * j + 64 * b:128 * j + 64 * (b + 1)]
                terms += [(o, T.dq[:, b, :], T.cq[:, r, 64 * j:64 * (j + 1)], 64, True), (o, T.dv[:, b, :], T.vs[:, r, 64 * j:64 * (j + 1)], 256, False)]
        mm("dg0%d" % r, terms, ["cq", "vs0", "vs1", "dq00", "dq01", "dq10", "dq11", "dw0", "dw1"], pk, [bk])
        act("da0%d" % r, T.da[:, :, r, 0:64], pd[:, 0:128], F.Identity, T.col[:, 0:1], 1.0, pk + ["col0"], ["da%d" % r], 128, [bk])
        act("db0%d" % r, T.db[:, r, :], pd[:, 128:256], F.Identity, T.col[:, 0:1], 1.0, pk + ["col0"], ["db%d" % r], 128, [bk])
    if GT:
        for h in range(2):
            o = T.px[:, 512 * (2 + h):512 * (3 + h)]
            mm("po%d" % h, [(o, T.i32[:, 0, :], T.w0[:, 1536 * h:1536 * (h + 1):3], 2048, True), (o, I4, T.ones[:], 512, False)],
               ["i320", "ones", "di10"] + wtok(0, 1536 * h, 1536 * (h + 1)), ["px%d" % (2 + h)], ["X%d" % (2 + h)])

    def offsets(t, r):
        for k in (1,) if t == 0 else (0, 1):
            nm = "%s%d%d" % ("vu"[k], t, r)
            terms = []
            for j, x in enumerate((seg(T.da, r), half(T.db, r))):
                o = T.pf[:, 256 + 128 * k + 64 * j:320 + 128 * k + 64 * j]
                terms += [(o, T.wm[:, 2 * k + b, :], x(b), 64, b == 0) for b in range(2)]
            mm("p" + nm, terms, ["da%d" % r, "db%d" % r, "wm%d" % (2 * k), "wm%d" % (2 * k + 1)], ["pq%d" % k], ["PF"])
            ts("o" + nm, off[t][:, 256 * r + 128 * k:256 * r + 128 * (k + 1)], T.pf[:, 256 + 128 * k:384 + 128 * k], -LOW * (49, CS + 1)[k], None, A.add, None,
               ["pq%d" % k], ["o" + nm], 128, ["PF"])

    for r in range(3):
        offsets(0, r)

    bank = [0]

    def nextbank():
        bank[0] = (bank[0] + 1) % (2 if GT else 4)
        return bank[0]

    for t in range(ST):
        last = t == ST - 1
        win = w[t][:, 0:W]
        wk = wtok(t) + ["wg%d" % t]
        for e in range(2):
            dma("td%d%d" % (t, e), "y", T.tab[e:128:16, :], T.da[e:128:2], ["da0", "da1", "da2", "dag"], ["tab%d" % e], 768 * CS, 64)

        def lst(r, k, a=0, b=64): return off[t][:, 256 * r + 64 * k + a:256 * r + 64 * k + b]
        cl = [(t + j) % 3 for j in range(3)]
        for r in cl:
            nm = "%d%d" % (t, r)
            c = slice(G * r, G * (r + 1))
            thr = -8.5
            if r == t:
                act("xa" + nm, T.xa4[:], win.indirect(lst(r, 0)), F.Identity, 4.0, 1.0, wk + ["ov" + nm], ["xa4"], GA * G)
            if str(r) in SB[t]:
                act("xb" + nm, T.xb[:], win.indirect(lst(r, 1)), F.Identity, 0.0, 1.0, wk + ["ov" + nm], ["xb"], GA * G)
                for h in range(2):
                    b = nextbank()
                    o = T.px[:, 512 * b:512 * (b + 1)]
                    mm("pb%s%d" % (nm, h), [(o, T.i32[:, 1, :], w[t][:, 1536 * h + r:1536 * (h + 1):3], 2048, True)], ["i321"] + wtok(t), ["px%d" % b], ["X%d" % b], closes=False)
                    mm("pc%s%d" % (nm, h), [(o, T.i32[:, 0, :], T.xb[:, 512 * h:512 * (h + 1)], 2048, True)], ["xb", "i320", "px%d" % b], ["px%d" % b], ["X%d" % b], opens=False)
                    act("cp%s%d" % (nm, h), T.cp[:, G * r + 512 * h:G * r + 512 * (h + 1)], o, F.Sign, 0.5, -1.0, ["px%d" % b], ["cp%d%d" % (r, h)], 512, ["X%d" % b])
                thr = -1.0
            else:
                x, xk = own(t, r, 0, G)
                tt("cp" + nm, T.cp[:, c], win.indirect(lst(r, 1)), x, A.is_le, wk + xk + ["ov" + nm], ["cp%d0" % r, "cp%d1" % r], GA * G)
            mm("vp" + nm, fold(T.pc, 128 * r, 0, T.cp, G * r), ["cp%d0" % r, "cp%d1" % r] + wk_[0], ["cnt%d" % r], ["PC"])
            act("G" + nm, T.gt[:, r, :], T.pc[:, 128 * r:128 * (r + 1)], F.Sign, thr, 1.0, ["cnt%d" % r], ["G%d" % r], 128, ["PC"])
            if r == t:
                tt("c2%d" % t, T.c2[:], win.indirect(lst(r, 1)), T.xa4[:], A.is_gt, wk + ["ov" + nm, "xa4"], ["c2"], GA * G)
                terms = []
                d = nextbank() if t else None
                pd, dk, db_ = (T.px, ["px%d" % d], "X%d" % d) if t else (T.pp, ["P"], "PP")
                d0 = 512 * d if t else 0
                for k, x in enumerate((seg(T.sd, r), half(T.db, r))):
                    for b in range(2):
                        o = pd[:, d0 + 128 * k + 64 * b:d0 + 128 * k + 64 * (b + 1)]
                        terms += [(o, I1, seg(T.da, r)(b), 64, True), (o, IM1, x(b), 64, False)]
                mm("D%d" % t, terms, ["da%d" % r, "db%d" % r, "sd", "di0", "di1"], dk, [db_])
                mm("v2%d" % t, fold(T.pc, 384, 0, T.c2, 0, [(IM48, half(T.gt, r))]), ["c2", "G%d" % r, "di5"] + wk_[0], ["cnt2"], ["PC"])
                chv = ht[t][:, :, r, 0:64]
                ts("ch%d" % t, chv, T.pc[:, 384:512], 56.5, None, A.is_gt, None, ["cnt2"], ["h%d" % t], 128, ["PC"])
                tt("E1%d" % t, et[t][:, :, r, 0:64], pd[:, d0:d0 + 128], chv, A.mult, dk + ["h%d" % t], ["e%d" % t], 128, [db_])
                dma("td%d4" % t, "y", T.tab[4:128:16, :], ht[t][0:128:2], ["h%d" % t], ["tab4"], 768 * CS, 64)
                for e in range(2):
                    dma("td%d%d" % (t, 2 + e), "y", T.tae[2 + e:128:16, :], et[t][e:128:2], ["e%d" % t], ["tab%d" % (2 + e)], 768 * CS, 64)
                tt("E2%d" % t, T.sw[:], pd[:, d0 + 128:d0 + 256], chv, A.mult, dk + ["h%d" % t], ["sw"], 128, [db_])
        n = G // HA[t]
        for h in range(HA[t]):
            for r in cl:
                nm = "%d%d%d" % (t, r, h)
                lo, hi = 3 * n * h, 3 * n * (h + 1)
                gav = T.ga[:, G * r + n * h:G * r + n * (h + 1)]
                gk = ["ga%d%d" % (r, k) for k in range(2) if HA[t] == 1 or k == h]
                x, xk = own(t, r, n * h, n * (h + 1))
                if GT and r == t:
                    bs = [2 + k for k in range(2) if HA[t] == 1 or k == h]
                    tt("ga" + nm, gav, T.xa4[:, n * h:n * (h + 1)], T.px[:, G + n * h:G + n * (h + 1)], A.subtract,
                       ["xa4"] + ["px%d" % b for b in bs], gk, n, ["X%d" % b for b in bs])
                else:
                    tt("ga" + nm, gav, win.indirect(lst(r, 0, n // 16 * h, n // 16 * (h + 1))), x, A.subtract, wk + xk + ["ov%d%d" % (t, r)], gk, GA * n)
                ts("cl" + nm, cc[t][:, lo + r:hi:3], gav, 2.0, 7.0, A.max, A.min, gk, ["cc" + nm], n // 2)
        if not last and XT[t]:
            r = t + 1
            for h in range(2):
                grow(t, "%dt%d" % (t, h), XT[t][h], slice(1536 * h + r, 1536 * (h + 1), 3), T.xt[:, 512 * h:512 * (h + 1)],
                     ["cc%d%d%d" % (t, r, h * HA[t] // 2)], ["xt%d" % h], 2 + h if GT else None)
        if last:
            for k in range(AD[-1]):
                c = slice(512 * k, 512 * (k + 1))
                dma("st_x%d" % k, "y", T.yx[:, c], w[t][:, c], wtok(t, c.start, c.stop), ["yx%d" % k], 128 * 2048)
            for h, (lo, hi) in enumerate(zip(AD, AD[1:])):
                c = slice(512 * lo, 512 * hi)
                op("ad%d" % h, "G", lambda q, c=c: q.dma_start(T.yx[:, c], cc[t][:, c], accum_op=A.add),
                   ["yx%d" % k for k in range(lo, hi)] + cck(t, range(lo, hi)), [], cost=(128 * 2048 * (hi - lo) * ACC, 128))
        if True:
            for k in range(AD[-1] if last else 0, 6):
                nm = "%d%d" % (t, k)
                c = slice(512 * k, 512 * (k + 1))
                out = (T.yxs if last else w[t + 1])[:, c]
                tok = ["w%d_%d" % (t + 1, k)]
                grow(t, nm, ADD[t][k], c, out, cck(t, [k]), tok)
                if last:
                    dma("st_x%d" % k, "y", T.yx[:, c], out, tok, [], 128 * 2048)
        if not last:
            ghosts(t + 1)
            for k in range(6):
                c = slice(512 * k, 512 * (k + 1))
                dma("xd%d%d" % (t + 1, k), "y", xs[t + 1][:, c], w[t + 1][:, c], ["w%d_%d" % (t + 1, k)] + ["iss%d" % (t + 1)] * (k >= XH[t]),
                    ["xs%d_%d" % (t + 1, k)], 128 * 2048)
        for r in [(t + 1 + j) % 3 for j in range(3)]:
            nm = "%d%d" % (t, r)
            turn = r == t
            for j in (1, 0):
                o = T.rg[:, G * (2 * r + j):G * (2 * r + j + 1)]
                src = (T.tae, T.tab)[j][:, 0:48 * CS].indirect(lst(r, 2 + j))
                tk = (["tab2", "tab3"], ["tab0", "tab1", "tab4"])[j]
                if "%d%d" % (r, j) in RV[t].split():
                    cp("R%s%d" % (nm, j), o, src, tk + ["ou" + nm], ["R%d%d" % (r, j)], GA * G)
                else:
                    act("R%s%d" % (nm, j), o, src, F.Copy, 0.0, 1.0, tk + ["ou" + nm], ["R%d%d" % (r, j)], GA * G)
            chs = seg(ht[t], r)
            hk = ["h%d" % t] if turn else []
            gr, s1, s2 = T.gt[:, r, :], T.sg[:, r, 0:128], T.sg[:, r, 128:256]
            pa, pb = T.pp[:, 0:128], T.py[:, 128 * r:128 * (r + 1)]
            xa, xb = T.xm[:, r, 0:128], T.xm[:, r, 128:256]
            mm("B" + nm, fold(T.py, 128 * r, 2, T.rg, G * (2 * r + 1), [(IF, half(T.gt, r))] + [(IM2F, chs)] * (2 * turn)),
               ["R%d1" % r, "G%d" % r, "di2", "di8"] + hk + wk_[2], ["Q%d" % r], ["PY"])
            act("S" + nm, s1, pb, F.Sign, 0.5 - LOW, 1.0, ["Q%d" % r], ["sa%d" % r], 128, ["PY"])
            act("U" + nm, s2, pb, F.Sign, -2.5 * FL - LOW, 1.0, ["Q%d" % r], ["sb%d" % r], 128, ["PY"])
            tt("mb" + nm, xb, pb, T.db[:, r, :], A.max, ["Q%d" % r, "db%d" % r], ["xmb%d" % r], 128, ["PY"])
            relu = str(r) in MA[t]
            mm("A" + nm, [(pa, IF, T.ones[:, 0:128], 128, True), (pa, IF, gr, 128, False)] + [(pa, IM1, T.db[:, r, :], 128, False)] * relu
               + fold(T.pp, 0, 1, T.rg, G * 2 * r, [(I1, seg(T.da, r))] + [(IM2F, chs)] * turn, own=False),
               ["R%d0" % r, "da%d" % r, "db%d" % r, "G%d" % r, "ones", "di0", "di1", "di2", "di8"] + hk + wk_[1], ["P"], ["PP"], closes=False)
            mm("C" + nm, [(pa, IMF, s1, 128, False)], ["sa%d" % r, "P", "di3"], ["P"], ["PP"])
            if relu:
                act("ma" + nm, xa, pa, F.Relu, 0.0, 1.0, ["P"], ["xma%d" % r], 128, ["PP"])
            else:
                tt("ma" + nm, xa, pa, T.db[:, r, :], A.max, ["P", "db%d" % r], ["xma%d" % r], 128, ["PP"])
            if last:
                for j in (1, 0):
                    d = j + 2 * (r % 2)
                    pv, pk, bk = T.px[:, 512 * d:512 * d + 64], ["px%d" % d], "X%d" % d

                    def part(l, x):
                        return [((T.px[:, 512 * d + 32 * u:512 * d + 32 * (u + 1)]), l(b), x(b, u), 64, False) for u in range(2) for b in range(2)]

                    def cols(buf, c0): return lambda b, u: buf[:, r, c0 + 64 * b + u:c0 + 64 * (b + 1):2]
                    up, dn, one = (lambda b: T.wf[:, 0, b, :]), (lambda b: T.wf[:, 1, b, :]), (lambda b: T.wm[:, b, :])
                    terms = [(pv, (IKA, IKB)[j], T.k49[:], 64, True)]
                    if j:
                        terms += part(dn, cols(T.sg, 0)) + 2 * part(dn, cols(T.sg, 128))
                        terms += part(one, lambda b, u: T.sw[:, 64 * b + u:64 * (b + 1):2]) * turn
                    else:
                        terms += part(up, cols(T.sg, 0)) + part(dn, cols(T.gt, 0)) + 2 * turn * part(up, lambda b, u: ht[t][:, b, r, u:64:2])
                        terms += part(one, cols(T.db, 0)) * relu
                    mm("fu%d%d" % (r, j), terms, ["db%d" % r, "k49", "di11", "di12", "wf0", "wf1", "wm0", "wm1", "sa%d" % r] + (["sb%d" % r] + ["sw"] * turn if j else ["G%d" % r] + hk),
                       pk, [bk], closes=False)
                    mm("fv%d%d" % (r, j), part(one, cols(T.xm, 128 * j)), ["xm%s%d" % ("ab"[j], r)] + pk, pk, [bk])
                    for u in range(2):
                        op("fx%d%d%d" % (r, j, u), "v", lambda q, r=r, j=j, u=u, d=d: q.transpose(
                            T.rawo[:, 2 * j:2 * j + 2, 48 * u + r:48 * (u + 1):3], T.px[:, 512 * d + 32 * u:512 * d + 32 * (u + 1)]), pk, ["ro%d%d%d" % (r, j, u)], [bk])
                continue
            fa, fb = T.pf[:, 0:128], T.pf[:, 128:256]
            mm("M" + nm, [(fb, I1, xb, 128, True), (fb, IMH, s1, 128, False), (fb, IMF, s2, 128, False)] + [(fb, I1, T.sw[:], 128, False)] * turn,
               ["xmb%d" % r, "sa%d" % r, "sb%d" % r, "di0", "di3", "di7"] + ["sw"] * turn, ["M"], ["PF"])
            terms = [(fa, IH, s1, 128, True), (fa, IMH, gr, 128, False)] + [(fa, I1, T.db[:, r, :], 128, False)] * relu
            terms += [(T.pf[:, 64 * b:64 * (b + 1)], IF, chs(b), 64, False) for b in range(2 * turn)] + [(fa, I1, xa, 128, False)]
            mm("N" + nm, terms, ["xma%d" % r, "sa%d" % r, "G%d" % r, "di0", "di2", "di4", "di7"] + hk + ["db%d" % r] * relu, ["N"], ["PF"])
            act("db%d%d" % (t + 1, r), T.db[:, r, :], fb, F.Identity, -1.5 * FL, 1.0, ["M"], ["db%d" % r], 128, ["PF"])
            act("da%d%d" % (t + 1, r), T.da[:, :, r, 0:64], fa, F.Identity, -FL, 1.0, ["N"], ["da%d" % r], 128, ["PF"])
            offsets(t + 1, r)
    for k in range(4):
        dma("st_p%d" % k, "ya"[k % 2], (T.ya, T.yb)[k // 2][k % 2::2, :], T.rawo[:, k, :], ["ro%d%d%d" % (r, k // 2, u) for r in range(3) for u in range(2)], [], 128 * 384)
    return ops


QUEUE = {"v": "v", "s": "s", "a": "s", "t": "t", "y": "y", "g": "g", "G": "g", "r": "g", "i": "g", "n": "n"}


def depend(seq, banks):
    wrote, read, bank, deps = {}, {}, {}, []
    for k, o in enumerate(seq):
        d = set()
        for x in o["rd"]:
            if x in wrote: d.add(wrote[x])
        for x in o["wr"]:
            if x in wrote: d.add(wrote[x])
            d.update(read.get(x, []))
        if banks:
            for b in o["banks"]:
                d.update(j for q, j in bank.setdefault(b, {}).items() if q != o["eng"])
                bank[b][o["eng"]] = k
        for x in o["rd"]:
            read.setdefault(x, []).append(k)
        for x in o["wr"]:
            wrote[x] = k; read[x] = []
        d.discard(k)
        deps.append(sorted(d))
    return deps


def times(o):
    e, c = o["eng"], o["cost"]
    if e in "ni":
        return 0.0, 0.0, 0.0
    if e in "yaGr":
        return {"y": 60.0, "a": 60.0, "G": 900.0, "r": 400.0}[e], (c[0] / 25.0 + 25.0 * c[1]) / 16, 1200.0
    return (0.0 if e == "t" else 30.0) + 0.83 * max(c, 64), 0.0, 80.0


def names(q):
    out = []
    for t, line in enumerate(q):
        for x in line.split():
            s = t - x.startswith("-")
            x = x.lstrip("-")
            for c, r in (("T", s), ("N", s + 1), ("O", s + 2)):
                x = x.replace("." + c, "%d%d" % (s, r % 3)).replace(":" + c, "%d%d" % (s + 1, r % 3))
            out.append(x.replace("#", str(s)).replace("+", str(s + 1)))
    return out


def place(ops, tm, before, rank, back):
    used, start = {}, {}
    for k in rank:
        o = ops[k]
        hold, move, lat = tm[k]
        whole = hold + move + lat
        need = [(QUEUE[o["eng"]], 0.0, hold, None)] + [(b, 0.0, whole, o["eng"]) for b in o["banks"]] + ([("d", hold + lat / 2, move, None)] if move else [])
        if back:
            need = [(r, whole - a - n, n, e) for r, a, n, e in need]
        t = max([0.0] + [start[j] + gap for j, gap in before[k].items()])
        moved = True
        while moved:
            moved = False
            for r, a, n, e in need:
                for lo, hi, who in used.get(r, []):
                    if lo < t + a + n - 1e-6 and t + a < hi - 1e-6 and (e is None or e != who):
                        t = hi - a; moved = True
        for r, a, n, e in need:
            if n:
                used.setdefault(r, []).append((t + a, t + a + n, e))
        start[k] = t
    return start


def order(ops):
    n = len(ops)
    tm = [times(o) for o in ops]
    deps = [{j: sum(tm[j]) for j in d} for d in depend(ops, False)]
    after = [{} for _ in ops]
    for k in range(n):
        for j in deps[k]:
            after[j][k] = sum(tm[k])
    index = {o["name"]: k for k, o in enumerate(ops)}
    for q in LISTS:
        line = [index[x] for x in names(q)]
        for j, k in zip(line, line[1:]):
            deps[k].setdefault(j, tm[j][0])
            after[j].setdefault(k, tm[j][0] + sum(tm[k]) - sum(tm[j]))
    way = [0.0] * n
    left, todo = [len(x) for x in after], [k for k in range(n) if not after[k]]
    for k in todo:
        way[k] = 1.0 + max([sum(tm[k])] + [way[j] + deps[j][k] for j in after[k]])
        for j in deps[k]:
            left[j] -= 1
            if not left[j]:
                todo.append(j)
    assert len(todo) == n, [ops[k]["name"] for k in range(n) if left[k]][-12:]
    rank = sorted(range(n), key=lambda k: -way[k])
    best = None
    for _ in range(TURNS):
        start = place(ops, tm, deps, rank, False)
        end = max(start[k] + sum(tm[k]) for k in range(n))
        if best is None or end < best[0]:
            best = (end, start, max(way))
        late = place(ops, tm, after, sorted(range(n), key=lambda k: (-start[k], way[k])), True)
        rank = sorted(range(n), key=lambda k: (-late[k] - sum(tm[k]), -way[k]))
    EST.append(best)
    return [ops[k] for k in sorted(range(n), key=lambda k: (best[1][k], -way[k]))]


def improve(ops, seq):
    n = len(ops)
    tm = [times(o) for o in ops]
    deps = depend(ops, False)
    anc = [0] * n
    for k in range(n):
        for j in deps[k]:
            anc[k] |= anc[j] | (1 << j)
    qn = ["vstygn".index(QUEUE[o["eng"]]) for o in ops]
    bn = {b: i for i, b in enumerate(sorted(set(b for o in ops for b in o["banks"])))}
    bk = [[3 * bn[b] for b in o["banks"]] for o in ops]
    other = [[b + e for b in bk[k] for e in range(3) if e != qn[k]] for k in range(n)]

    def run(seq):
        free, who, bank, fin, why = [0.0] * 7, [n] * 7, [n] * (3 * len(bn)), [0.0] * (n + 1), [0] * n
        for k in seq:
            hold, move, lat = tm[k]
            q = qn[k]
            t, y = free[q], who[q]
            for b in other[k]:
                if fin[bank[b]] > t:
                    y = bank[b]; t = fin[y]
            for j in deps[k]:
                if fin[j] > t:
                    t, y = fin[j], j
            t += hold
            free[q], who[q] = t, k
            if move:
                t += lat / 2
                if free[6] > t:
                    t, y = free[6], who[6]
                free[6], who[6] = t + move, k
                fin[k] = t + move + lat / 2
            else:
                fin[k] = t + lat
            why[k] = y
            for b in bk[k]:
                bank[b + q] = k
        return fin, why

    x = SEED
    fin, why = run(seq)
    now = max(fin)
    best = (now, seq)
    for it in range(SWAPS):
        k, pairs = fin.index(now), []
        while k != n:
            j = why[k]
            if j != n and not anc[k] >> j & 1:
                pairs.append((j, k))
            k = j
        x = (x * 6364136223846793005 + 1442695040888963407) % 2 ** 64
        u, v = pairs[(x >> 40) % len(pairs)]
        pu, pv = seq.index(u), seq.index(v)
        part = seq[pu:pv + 1]
        if x >> 33 & 1:
            go = [k == v or anc[v] >> k & 1 for k in part]
        else:
            go = [not (k == u or anc[k] >> u & 1) for k in part]
        new = seq[:pu] + [k for k, y in zip(part, go) if y] + [k for k, y in zip(part, go) if not y] + seq[pv + 1:]
        f, y = run(new)
        end = max(f)
        if end <= now + (HEAT * (1 - it / SWAPS) ** 2 + 5.0) * -math.log(((x >> 8) % 2 ** 20 + 1) / 2 ** 20):
            seq, fin, why, now = new, f, y, end
            if end < best[0]:
                best = (end, new)
    EST.append((best[0], [f - sum(t) for f, t in zip(run(best[1])[0], tm)], 0))
    return best[1]


FOUND = {}
ORDER = """
ld_x0 ld_snd ld_x1 ld_x2 ld_x3 ones tae0 win0 dv0 sd0 pi t8a di0 tc pj0 wm0 wm100 pj1 dv1 di5 dq11 dv2 col1 sd1 di2 k49 zh0 snd16 ze0 col0 cv1 cv0 gg00 di10 t8c sdc ld_p3 ld_p1 wm110 wm000 t8b ld_p0 ld_p2 dq10 dq01 tab0 gg01 sh01 sh21 sh20 sh10 sh11 sh00 tr1 tr2 tr0 wm111 sd00 sd01 dq00 vs1 vs0 cq di1 di6 win01 i321 win10 i320 arr0 cv3 ov02 cv2 ov01 ov00 win20 win21 cp00 wm101 wm010 ze1 wm011 wm001 zh1 zh2 ze2 win00 di11 xa00 dg02 dg01 dg00 da02 db00 po1 db02 dag win11 da00 vp00 c20 pu00 ga001 ou00 ga020 da01 G00 db01 gm di12 wf1 wf0 di7 D0 v20 pu01 po0 ch0 ga010 E10 ou01 pu02 cl001 cl020 ou02 ga000 cp01 cl000 cl010 ga011 ga021 cl011 cl021 td01 td00 td04 di4 di3 di9 di8 R011 R021 pr0t1 pr0t0 td02 td03 vp01 G01 ac01 B01 ac00 R010 E20 mb01 A01 xc00 xc01 gg11 S01 C01 ma01 cp02 U01 gg10 ac0t0 M01 N01 ac03 da11 db11 R020 xc0t0 xc03 ac0t1 pu11 xc0t1 ac02 pv11 xc02 ac05 ac04 vp02 ov11 xc05 xc04 sd11 sd10 arr1 G02 iss1 D1 B02 xa11 S02 U02 R001 xd13 xd15 xd12 xd10 xd14 xd11 ou11 cp11 A02 C02 vp11 ga110 mb02 cl110 ma02 M02 N02 db12 da12 G11 R000 B00 pv12 c21 ga111 ov12 cl111 v21 pu12 mb00 ch1 ou12 E11 ga120 A00 S00 U00 C00 ma00 M00 N00 da10 db10 pr1t0 pv10 pr1t1 td12 td13 td14 td10 td11 R120 cl120 cp12 E21 ga121 ov10 cl121 ga100 ga101 cl100 pu10 ac1t0 ac1t1 vp12 R121 xc1t1 G12 ac11 xc1t0 cl101 B12 xc11 ou10 gg20 mb12 cp10 S12 U12 gg21 A12 ac13 C12 M12 ac10 ma12 vp10 xc13 ac15 N12 R101 xc10 ac12 G10 db22 da22 R100 xc15 B10 pu22 xc12 ac14 mb10 ou22 pv22 sd20 sd21 iss2 arr2 xc14 ov22 cp22 U10 S10 xa22 A10 M10 D2 C10 ma10 N10 vp22 c22 xd22 xd23 xd20 xd21 xd24 xd25 st_x0 R111 G22 da20 db20 R110 v22 pu20 pv20 B11 A11 ga220 ga221 ch2 ov20 E12 cl220 ou20 cl221 mb11 ga200 S11 U11 C11 ma11 M11 N11 da21 db21 pu21 pv21 cp20 ov21 cl200 ga210 ou21 cl210 vp20 td24 td22 td23 st_x1 td21 td20 st_x2 st_x4 st_x5 st_x3 R200 G20 R201 cp21 R211 R221 A20 B20 vp21 S20 U20 G21 C20 fu01 mb20 ma20 ga201 ga211 cl201 cl211 B22 B21 R210 U21 S21 fv01 A21 E22 fu10 C21 fu00 fu11 ma21 fx010 mb21 mb22 R220 S22 U22 ad0 A22 fv00 fx011 fu21 fv11 C22 fv21 fx000 fx001 fx111 fx110 fx211 fx210 ad1 ad2 fu20 fv10 ma22 fx101 fx100 fv20 fx201 fx200 st_p3 st_p2 st_p0 st_p1
"""


def rank_program(g, core, T, topo):
    if T.rank_of(core) is None:
        return
    ops = build(T, topo, core)
    if not FOUND:
        index = {o["name"]: k for k, o in enumerate(ops)}
        FOUND[0] = [index[x] for x in ORDER.split()]
        assert sorted(FOUND[0]) == list(range(len(ops)))
    seq = [ops[k] for k in FOUND[0]]
    deps = depend(seq, True)
    qs = {"v": g.vector, "s": g.scalar, "t": g.tensor, "y": g.sync, "g": g}
    needed = set(j for k, d in enumerate(deps) if seq[k]["eng"] != "n" for j in d)
    done, count, waited, sent = {}, {"v": 0, "s": 0, "t": 0, "g": 0}, {}, 0
    for k, o in enumerate(seq):
        e = o["eng"]
        if e == "n":
            done[k] = (o["name"], o["cost"])
            continue
        if e == "i":
            if k in needed:
                g.sem_inc(T.sem[o["name"]], 1); done[k] = (o["name"], 1)
            continue
        qn = QUEUE[e]
        need = {}
        for j in deps[k]:
            if seq[j]["eng"] == "r" or (e == "t" and seq[j]["eng"] == "t" and not set(seq[j]["wr"]) - set(o["rd"])):
                continue
            s, v = done[j]
            need[s] = max(need.get(s, 0), v)
        for s, v in need.items():
            if waited.get((qn, s), 0) < v:
                qs[qn].wait_ge(T.sem[s], v); waited[(qn, s)] = v
        ins = o["fn"](qs[qn])
        if e == "r":
            sent += len(topo.engines(core, T.cores[(T.rank_of(core) - 1) % len(T.cores)]))
        elif e in "yaG":
            ins.then_inc(T.sem[o["name"]], 16); done[k] = (o["name"], 16)
        elif k in needed:
            count[e] += 1
            ins.then_inc(T.sem["q" + e], 1); done[k] = ("q" + e, count[e])
    g.wait_ge(T.sem.sent, sent)
    for k, o in enumerate(seq):
        if o["eng"] in "yaG" and k not in needed:
            g.wait_ge(T.sem[o["name"]], 16)
    for e, v in count.items():
        if max([x for (q, s), x in waited.items() if s == "q" + e] + [0]) < v:
            g.wait_ge(T.sem["q" + e], v)
